import numpy as np
import ml_dtypes


def mxq(x, axis, fmt="e4m3"):
    dtype, down = {"e4m3": (ml_dtypes.float8_e4m3fn, 7), "e5m2": (ml_dtypes.float8_e5m2, 14)}[fmt]
    v = np.moveaxis(np.asarray(x, np.float32).astype(ml_dtypes.bfloat16).astype(np.float64), axis, -1)
    blocks = v.reshape(v.shape[:-1] + (-1, 32))
    amax = np.abs(blocks).max(-1, keepdims=True)
    byte = np.maximum(np.where(amax > 0, np.frexp(amax)[1] - 1 + 127, 0) - down, 1)
    scale = np.exp2(byte - 127.0)
    codes = (blocks / scale).astype(np.float32).astype(dtype).astype(np.float64)
    return np.moveaxis((codes * scale).reshape(v.shape), -1, axis)


WIDE = False


def mx_kscale(k):
    if not WIDE:
        return np.ones(k)
    levels = np.array([24, -24, 12, -12, 0])
    if k % 512:
        return np.exp2(np.random.permutation(np.resize(levels, k // 32))).repeat(32)
    a = np.empty((k // 512, 16))
    for p in range(k // 512):
        a[p, :8] = np.random.permutation(np.resize(levels, 8))
        for g in range(8):
            far = levels[np.abs(levels - a[p, g]) >= 10]
            a[p, g + 8] = far[np.random.randint(len(far))]
    return np.exp2(a.ravel()).repeat(32)


def f64(x):
    return np.asarray(x).astype(np.float64)


def striped8(idx):
    return np.concatenate([v.reshape(-1, 16).T for v in idx]).astype(np.uint16)


def unstriped8(offs):
    return np.stack([offs[16 * g:16 * g + 16].T.reshape(-1) for g in range(8)]).astype(np.int64)


E2M1 = np.array([0.0, 0.5, 1.0, 1.5, 2.0, 3.0, 4.0, 6.0, -0.0, -0.5, -1.0, -1.5, -2.0, -3.0, -4.0, -6.0])


def pack_weight(w, fmt):
    k, n = w.shape
    w = f64(np.asarray(w, np.float32).astype(ml_dtypes.bfloat16)).reshape(k // 32, 32, n)
    amax = np.abs(w).max(1)
    if fmt == "e4m3":
        byte = np.frexp(amax)[1] - 1 + 127 - 7
    else:
        mant, ex = np.frexp(amax / 6.0)
        byte = np.where(mant > 0.5, ex, ex - 1) + 127
    byte = np.clip(np.where(amax > 0, byte, 1), 1, 254)
    scaled = (w * np.exp2(127.0 - byte)[:, None, :]).reshape(k, n).astype(np.float32)
    by_word = np.ascontiguousarray(scaled.reshape(k // 512, 128, 4, n).transpose(0, 1, 3, 2))
    if fmt == "e4m3":
        words = by_word.astype(ml_dtypes.float8_e4m3fn).view(np.uint8)
    else:
        c = by_word.astype(ml_dtypes.float4_e2m1fn).view(np.uint8) & 0xF
        words = (c[..., 0::2] | (c[..., 1::2] << 4)).reshape(k // 512, 128, 2 * n)
    return np.ascontiguousarray(words), np.ascontiguousarray(byte.astype(np.uint8).reshape(k // 512, 16, n))


def unpack_weight(words, scales, fmt):
    g, _, n = scales.shape
    words = np.ascontiguousarray(words).reshape(g, 128, n, -1)
    if fmt == "e4m3":
        vals = words.view(ml_dtypes.float8_e4m3fn).astype(np.float64)
    else:
        nib = np.empty((g, 128, n, 4), np.uint8)
        nib[..., 0::2] = words & 0xF
        nib[..., 1::2] = words >> 4
        vals = E2M1[nib]
    vals = vals * np.repeat(np.exp2(scales.astype(np.float64) - 127.0), 8, axis=1)[..., None]
    return vals.transpose(0, 1, 3, 2).reshape(g * 512, n)


def planes(y):
    n, m = y.shape
    v = y.astype(np.float32).astype(ml_dtypes.bfloat16).astype(np.float64).reshape(n // 32, 32, m)
    top = np.abs(v).max(1)
    byte = np.clip(np.where(top > 0, np.frexp(top)[1] - 1 + 127 - 7, 1), 1, 254)
    codes = (v * np.exp2(127.0 - byte)[:, None, :]).reshape(n, m).astype(np.float32).astype(ml_dtypes.float8_e4m3fn).view(np.uint8)
    words = codes.reshape(n // 512, 128, 4, m).transpose(0, 1, 3, 2)
    return np.ascontiguousarray(words), np.ascontiguousarray(byte.astype(np.uint8).reshape(n // 512, 16, m))


def sigm(f):
    return 1.0 / (1.0 + np.exp(-np.maximum(f, -700.0)))


K, N, T, J = 1024, 512, 2048, 1024


def setup_inputs():
    n = np.random.standard_normal
    s = mx_kscale(K)[:, None]
    p_wv4 = pack_weight(n((K, N)) / np.sqrt(K) / s, "e2m1")
    return {
        "xT": (n((K, T)) * s).astype(np.float32),
        "wgt": np.repeat(np.random.uniform(0.5, 2.0, (8, J)), 16, axis=0).astype(np.float32),
        "wk": (n((K, N)) / np.sqrt(K) / s).astype(np.float32),
        "wv4_words": p_wv4[0],
        "wv4_scales": p_wv4[1],
        "wvd": (0.4 * (n((K, N)) / np.sqrt(K) / s)).astype(np.float32),
        "st": (n((N, J))).astype(np.float32),
        "offs": striped8(np.stack([np.random.permutation(T)[:J] for _ in range(8)])),
    }


def reference(xT, wgt, wk, wv4_words, wv4_scales, wvd, st, offs):
    idx = unstriped8(offs)
    rows = np.arange(K)
    xg = f64(wgt)[rows // 4 % 128] * f64(xT)[rows[:, None], idx[rows % 512 // 64]]
    xT_ = mxq(xg, 0, "e4m3")
    wk_ = mxq(f64(wk), 0, "e4m3")
    wv4_ = unpack_weight(wv4_words, wv4_scales, "e2m1")
    wvd_ = mxq(f64(wvd), 0, "e4m3")
    ke = wk_.T @ xT_
    ve = wv4_.T @ xT_ + wvd_.T @ xT_
    gate = sigm(ke * f64(st))
    out_0 = gate * ve
    return (out_0,) + planes(out_0)

@@ -1,0 +1,231 @@
+from contextlib import ExitStack
+
+import concourse.mybir as mybir
+
+K, N, T, J = 1024, 512, 2048, 1024
+FLOPS = 3 * 2 * K * N * J
+
+F32 = mybir.dt.float32
+BF16 = mybir.dt.bfloat16
+I32 = mybir.dt.int32
+U32 = mybir.dt.uint32
+U16 = mybir.dt.uint16
+U8 = mybir.dt.uint8
+FP8X4 = mybir.dt.float8_e4m3fn_x4
+FP4X4 = mybir.dt.float4_e2m1fn_x4
+MULT = mybir.AluOpType.mult
+SIGMOID = mybir.ActivationFunctionType.Sigmoid
+
+P = 128
+PACK = 4
+K_PASS = P * PACK
+PASSES = K // K_PASS
+HALF = J // 2
+QUARTER = J // 4
+FP4_N = 128
+
+
+def copy_on(nc, engine, out, in_):
+    if engine == "scalar":
+        nc.scalar.copy(out=out, in_=in_)
+    else:
+        nc.vector.tensor_copy(out=out, in_=in_)
+
+
+def interleave(nc, engine, out, rows):
+    copy_on(
+        nc,
+        engine,
+        out.rearrange("p (c i t) -> p c t i", i=4, t=PACK),
+        rows.rearrange("p t (c i) -> p c t i", i=4),
+    )
+
+
+def deal_weight(nc, engine, out, raw, t0, t1):
+    copy_on(
+        nc,
+        engine,
+        out.rearrange("p (t m j) -> p m j t", t=t1 - t0, j=PACK),
+        raw.rearrange("p j (m t) -> p m j t", t=PACK)[:, :, :, t0:t1],
+    )
+
+
+def tile_list_dl_sigP_kernel(
+    tc, xT, wgt, wk, wv4_words, wv4_scales, wvd, st, offs, out_0, out_1, out_2
+):
+    nc = tc.nc
+    with ExitStack() as ctx:
+        keep = ctx.enter_context(tc.tile_pool(name="keep", bufs=1))
+        psum = ctx.enter_context(tc.psum_pool(name="psum", bufs=1))
+
+        offsets = keep.tile([P, J // 16], U16, name="offsets")
+        nc.sync.dma_start(offsets[:], offs)
+
+        v4_raw = keep.tile([P, PASSES, 2 * N], U8, name="v4_raw")
+        nc.sync.dma_start(
+            out=v4_raw[:].bitcast(I32),
+            in_=wv4_words.bitcast(I32).rearrange("a p w -> p a w"),
+        )
+        v4s_raw = keep.tile([P, PASSES, N], U8, name="v4s_raw")
+        nc.gpsimd.memset(v4s_raw[:].bitcast(I32), 0)
+        for q in range(4):
+            nc.scalar.dma_start(
+                out=v4s_raw[32 * q : 32 * q + 4, :, :].bitcast(I32),
+                in_=wv4_scales[:, 4 * q : 4 * q + 4, :].bitcast(I32).rearrange("a r w -> r a w"),
+            )
+
+        wgt_sb = [keep.tile([P, HALF], F32, name="wgt%d" % h) for h in range(2)]
+        planes = [keep.tile([P, T], F32, name="plane%d" % r) for r in range(PASSES * PACK)]
+        x_rows = xT.rearrange("(a p i) t -> a i p t", p=P, i=PACK)
+        nc.sync.dma_start(out=wgt_sb[0][:], in_=wgt[:, 0:HALF])
+        nc.sync.dma_start(out=planes[0][:], in_=x_rows[0, 0])
+        nc.sync.dma_start(out=wgt_sb[1][:], in_=wgt[:, HALF:J])
+        for r in range(1, PASSES * PACK):
+            nc.sync.dma_start(out=planes[r][:], in_=x_rows[r // PACK, r % PACK])
+
+        wk_raw = [keep.tile([P, PACK, N], F32, name="wk_raw%d" % a) for a in range(PASSES)]
+        wd_raw = [keep.tile([P, PACK, N], F32, name="wd_raw%d" % a) for a in range(PASSES)]
+        y = [keep.tile([P, PACK, QUARTER], F32, name="y%d" % q) for q in range(4)]
+        wk_rows = wk.rearrange("(a p j) n -> a p j n", p=P, j=PACK)
+        wd_rows = wvd.rearrange("(a p j) n -> a p j n", p=P, j=PACK)
+        st_rows = st.rearrange("(p t) j -> p t j", t=PACK)
+        out_rows = out_0.rearrange("(p t) j -> p t j", t=PACK)
+        for a in range(PASSES):
+            nc.sync.dma_start(out=wk_raw[a][:], in_=wk_rows[a])
+        for q in range(3):
+            nc.sync.dma_start(out=y[q][:], in_=st_rows[:, :, q * QUARTER : (q + 1) * QUARTER])
+        for a in range(PASSES):
+            nc.sync.dma_start(out=wd_raw[a][:], in_=wd_rows[a])
+        for q in range(3, 4):
+            nc.sync.dma_start(out=y[q][:], in_=st_rows[:, :, q * QUARTER : (q + 1) * QUARTER])
+
+        v4_codes = keep.tile([P, PASSES, 2 * N], U8, name="v4_codes", align_bytes=64)
+        v4_scales = keep.tile([P, PASSES, N], U8, name="v4_scales", align_bytes=64)
+        nc.vector.tensor_copy(
+            out=v4_codes[:].bitcast(U16).rearrange("p a (t m) -> p a m t", t=PACK),
+            in_=v4_raw[:].bitcast(U16).rearrange("p a (m t) -> p a m t", t=PACK),
+        )
+        nc.vector.tensor_copy(
+            out=v4_scales[:].rearrange("p a (t m) -> p a m t", t=PACK),
+            in_=v4s_raw[:].rearrange("p a (m t) -> p a m t", t=PACK),
+        )
+
+        x_codes = {}
+        x_scales = {}
+        for a in range(PASSES):
+            picked = [keep.tile([P, PACK, HALF], F32, name="picked%d%d" % (a, h)) for h in range(2)]
+            for i in range(PACK):
+                for h in range(2):
+                    nc.vector.tensor_tensor(
+                        out=picked[h][:, i, :],
+                        in0=planes[a * PACK + i][:].indirect(offsets[:, 32 * h : 32 * (h + 1)]),
+                        in1=wgt_sb[h][:],
+                        op=MULT,
+                    )
+            for h in range(2):
+                x_bf = keep.tile([P, PACK * HALF], BF16, name="x_bf%d%d" % (a, h), align_bytes=64)
+                interleave(nc, ("scalar", "scalar", "scalar", "vector")[2 * a + h], x_bf[:], picked[h][:])
+                x_codes[a, h] = keep.tile([P, HALF], U32, name="x_codes%d%d" % (a, h), align_bytes=64)
+                x_scales[a, h] = keep.tile([P, HALF], U8, name="x_scales%d%d" % (a, h), align_bytes=64)
+                nc.vector.quantize_mx(out=x_codes[a, h][:].bitcast(FP8X4), scales=x_scales[a, h][:], in_=x_bf[:])
+
+        def quantise_weight(name, raw, engines):
+            codes, scales = [], []
+            for u in range(2):
+                w_bf = keep.tile([P, 2 * N], BF16, name="%s_bf%d" % (name, u), align_bytes=64)
+                deal_weight(nc, engines[u], w_bf[:], raw[:], 2 * u, 2 * u + 2)
+                c = keep.tile([P, 2 * P], U32, name="%s_codes%d" % (name, u), align_bytes=64)
+                s = keep.tile([P, 2 * P], U8, name="%s_scales%d" % (name, u), align_bytes=64)
+                nc.vector.quantize_mx(out=c[:].bitcast(FP8X4), scales=s[:], in_=w_bf[:])
+                codes.append(c)
+                scales.append(s)
+            return codes, scales
+
+        def e4m3_pass(bank, w, a, q, u, start, stop):
+            codes, scales = w
+            h = q // 2
+            cols = slice((q % 2) * QUARTER, (q % 2 + 1) * QUARTER)
+            for v in range(2):
+                nc.tensor.matmul_mx(
+                    out=bank[:, v, :],
+                    lhsT=codes[u][:, v * P : (v + 1) * P].bitcast(FP8X4),
+                    lhsT_scale=scales[u][:, v * P : (v + 1) * P],
+                    rhs=x_codes[a, h][:, cols].bitcast(FP8X4),
+                    rhs_scale=x_scales[a, h][:, cols],
+                    start=start and v == 0,
+                    stop=stop and v == 1,
+                )
+
+        def e2m1_pass(bank, a, q, u, start):
+            h = q // 2
+            for v in range(2):
+                t = 2 * u + v
+                for e in range(QUARTER // FP4_N):
+                    c0 = (q % 2) * QUARTER + e * FP4_N
+                    nc.tensor.matmul_mx(
+                        out=bank[:, v, e * FP4_N : (e + 1) * FP4_N],
+                        lhsT=v4_codes[:, a, 2 * P * t : 2 * P * (t + 1)].bitcast(FP4X4),
+                        lhsT_scale=v4_scales[:, a, P * t : P * (t + 1)],
+                        rhs=x_codes[a, h][:, c0 : c0 + FP4_N].bitcast(FP8X4),
+                        rhs_scale=x_scales[a, h][:, c0 : c0 + FP4_N],
+                        start=start and v == 0 and e == 0,
+                        stop=False,
+                    )
+
+        wk_q = [quantise_weight("wk%d" % a, wk_raw[a], (("vector", "vector"), ("scalar", "scalar"))[a]) for a in range(PASSES)]
+        ke = {}
+        for q in range(4):
+            for u in range(2):
+                ke[q, u] = psum.tile([P, 2, QUARTER], F32, name="ke", tag="bank%d%d" % (q, u))
+        for a in range(PASSES):
+            for q in range(4):
+                for u in range(2):
+                    e4m3_pass(ke[q, u], wk_q[a], a, q, u, a == 0, a == PASSES - 1)
+
+        ve = {}
+
+        def gate(q):
+            for u in range(2):
+                rows = y[q][:, 2 * u : 2 * u + 2, :]
+                nc.vector.tensor_tensor(out=rows, in0=ke[q, u][:], in1=rows, op=MULT)
+            nc.scalar.activation(out=y[q][:], in_=y[q][:], func=SIGMOID)
+            for u in range(2):
+                ve[q, u] = psum.tile([P, 2, QUARTER], F32, name="ve", tag="bank%d%d" % (q, u))
+                for a in range(PASSES):
+                    e2m1_pass(ve[q, u], a, q, u, a == 0)
+
+        y_codes = [keep.tile([P, QUARTER], U32, name="y_codes%d" % q, align_bytes=64) for q in range(4)]
+        y_scales = keep.tile([P, J], U8, name="y_scales", align_bytes=64)
+        words_out = out_1.rearrange("a p j i -> p (a j i)").bitcast(I32)
+
+        def finish(q):
+            cols = slice(q * QUARTER, (q + 1) * QUARTER)
+            for u in range(2):
+                rows = y[q][:, 2 * u : 2 * u + 2, :]
+                nc.vector.tensor_tensor(out=rows, in0=ve[q, u][:], in1=rows, op=MULT)
+            nc.sync.dma_start(out=out_rows[:, :, cols], in_=y[q][:])
+            y_bf = keep.tile([P, PACK * QUARTER], BF16, name="y_bf%d" % q, align_bytes=64)
+            interleave(nc, ("scalar", "scalar", "scalar", "scalar")[q], y_bf[:], y[q][:])
+            nc.vector.quantize_mx(out=y_codes[q][:].bitcast(FP8X4), scales=y_scales[:, cols], in_=y_bf[:])
+            nc.sync.dma_start(out=words_out[:, cols], in_=y_codes[q][:].bitcast(I32))
+
+        for q in range(3):
+            gate(q)
+        wd_q = [quantise_weight("wd%d" % a, wd_raw[a], (("vector", "scalar"), ("vector", "scalar"))[a]) for a in range(PASSES)]
+        for a in range(PASSES):
+            for q in range(3):
+                for u in range(2):
+                    e4m3_pass(ve[q, u], wd_q[a], a, q, u, False, a == PASSES - 1)
+        for q in range(3, 4):
+            gate(q)
+            for u in range(2):
+                for a in range(PASSES):
+                    e4m3_pass(ve[q, u], wd_q[a], a, q, u, False, a == PASSES - 1)
+        for q in range(4):
+            finish(q)
+        for q in range(4):
+            queue = nc.sync if q % 2 == 0 else nc.scalar
+            queue.dma_start(
+                out=out_2[0, 4 * q : 4 * q + 4, :].bitcast(I32),
+                in_=y_scales[32 * q : 32 * q + 4, :].bitcast(I32),
+            )

@@ -18,35 +18,19 @@ SIGMOID = mybir.ActivationFunctionType.Sigmoid
 
 P = 128
 PACK = 4
-K_PASS = P * PACK
-PASSES = K // K_PASS
+PASSES = K // (P * PACK)
+QUADRANTS = 4
+LIST_ROWS = 16
+LINE = 4
 HALF = J // 2
 QUARTER = J // 4
-FP4_N = 128
+MX_ALIGN = 64
 
 
-def copy_on(nc, engine, out, in_):
-    if engine == "scalar":
-        nc.scalar.copy(out=out, in_=in_)
-    else:
-        nc.vector.tensor_copy(out=out, in_=in_)
-
-
-def interleave(nc, engine, out, rows):
-    copy_on(
-        nc,
-        engine,
-        out.rearrange("p (c i t) -> p c t i", i=4, t=PACK),
-        rows.rearrange("p t (c i) -> p c t i", i=4),
-    )
-
-
-def deal_weight(nc, engine, out, raw, t0, t1):
-    copy_on(
-        nc,
-        engine,
-        out.rearrange("p (t m j) -> p m j t", t=t1 - t0, j=PACK),
-        raw.rearrange("p j (m t) -> p m j t", t=PACK)[:, :, :, t0:t1],
+def interleave(copy, out, rows):
+    copy(
+        out=out.rearrange("p (b c i) -> p b i c", c=LINE, i=PACK),
+        in_=rows.rearrange("p i (b c) -> p b i c", c=LINE),
     )
 
 
@@ -55,177 +39,185 @@ def tile_list_dl_sigP_kernel(
 ):
     nc = tc.nc
     with ExitStack() as ctx:
-        keep = ctx.enter_context(tc.tile_pool(name="keep", bufs=1))
+        sbuf = ctx.enter_context(tc.tile_pool(name="sbuf", bufs=1))
         psum = ctx.enter_context(tc.psum_pool(name="psum", bufs=1))
 
-        offsets = keep.tile([P, J // 16], U16, name="offsets")
+        def mx_tiles(name, width):
+            codes = sbuf.tile([P, width], U32, name=name + "_codes", align_bytes=MX_ALIGN)
+            scales = sbuf.tile([P, width], U8, name=name + "_scales", align_bytes=MX_ALIGN)
+            return codes, scales
+
+        offsets = sbuf.tile([P, J // LIST_ROWS], U16, name="offsets")
         nc.sync.dma_start(offsets[:], offs)
 
-        v4_raw = keep.tile([P, PASSES, 2 * N], U8, name="v4_raw")
-        nc.sync.dma_start(
-            out=v4_raw[:].bitcast(I32),
-            in_=wv4_words.bitcast(I32).rearrange("a p w -> p a w"),
-        )
-        v4s_raw = keep.tile([P, PASSES, N], U8, name="v4s_raw")
-        nc.gpsimd.memset(v4s_raw[:].bitcast(I32), 0)
-        for q in range(4):
+        v4_words_in = sbuf.tile([P, PASSES, 2 * N], U8, name="v4_words_in")
+        nc.sync.dma_start(out=v4_words_in[:].bitcast(I32), in_=wv4_words.bitcast(I32).rearrange("a p w -> p a w"))
+        v4_scales_in = sbuf.tile([P, PASSES, N], U8, name="v4_scales_in")
+        nc.vector.memset(v4_scales_in[:].bitcast(I32), 0)
+        for quad in range(QUADRANTS):
             nc.scalar.dma_start(
-                out=v4s_raw[32 * q : 32 * q + 4, :, :].bitcast(I32),
-                in_=wv4_scales[:, 4 * q : 4 * q + 4, :].bitcast(I32).rearrange("a r w -> r a w"),
+                out=v4_scales_in[32 * quad : 32 * quad + 4, :, :].bitcast(I32),
+                in_=wv4_scales[:, 4 * quad : 4 * quad + 4, :].bitcast(I32).rearrange("a r w -> r a w"),
             )
 
-        wgt_sb = [keep.tile([P, HALF], F32, name="wgt%d" % h) for h in range(2)]
-        planes = [keep.tile([P, T], F32, name="plane%d" % r) for r in range(PASSES * PACK)]
-        x_rows = xT.rearrange("(a p i) t -> a i p t", p=P, i=PACK)
-        nc.sync.dma_start(out=wgt_sb[0][:], in_=wgt[:, 0:HALF])
-        nc.sync.dma_start(out=planes[0][:], in_=x_rows[0, 0])
-        nc.sync.dma_start(out=wgt_sb[1][:], in_=wgt[:, HALF:J])
-        for r in range(1, PASSES * PACK):
-            nc.sync.dma_start(out=planes[r][:], in_=x_rows[r // PACK, r % PACK])
+        warm = sbuf.tile([P, 2], F32, name="warm")
+        nc.vector.memset(warm[:, 0:1], 0.0)
+        nc.scalar.activation(out=warm[:, 1:2], in_=warm[:, 0:1], func=SIGMOID)
 
-        wk_raw = [keep.tile([P, PACK, N], F32, name="wk_raw%d" % a) for a in range(PASSES)]
-        wd_raw = [keep.tile([P, PACK, N], F32, name="wd_raw%d" % a) for a in range(PASSES)]
-        y = [keep.tile([P, PACK, QUARTER], F32, name="y%d" % q) for q in range(4)]
-        wk_rows = wk.rearrange("(a p j) n -> a p j n", p=P, j=PACK)
-        wd_rows = wvd.rearrange("(a p j) n -> a p j n", p=P, j=PACK)
+        wgt_sb = sbuf.tile([P, J], F32, name="wgt_sb")
+        x_in = [sbuf.tile([P, T], F32, name="x_in%d" % r) for r in range(PASSES * PACK)]
+        wk_in = [sbuf.tile([P, PACK, N], F32, name="wk_in%d" % a) for a in range(PASSES)]
+        wd_in = [sbuf.tile([P, PACK, N], F32, name="wd_in%d" % a) for a in range(PASSES)]
+        gate = {(h, u): sbuf.tile([P, 2, HALF], F32, name="gate%d%d" % (h, u)) for h in range(2) for u in range(2)}
+        x_rows = xT.rearrange("(a p i) c -> a i p c", p=P, i=PACK)
+        wk_rows = wk.rearrange("(a p i) n -> a p i n", p=P, i=PACK)
+        wd_rows = wvd.rearrange("(a p i) n -> a p i n", p=P, i=PACK)
         st_rows = st.rearrange("(p t) j -> p t j", t=PACK)
         out_rows = out_0.rearrange("(p t) j -> p t j", t=PACK)
-        for a in range(PASSES):
-            nc.sync.dma_start(out=wk_raw[a][:], in_=wk_rows[a])
-        for q in range(3):
-            nc.sync.dma_start(out=y[q][:], in_=st_rows[:, :, q * QUARTER : (q + 1) * QUARTER])
-        for a in range(PASSES):
-            nc.sync.dma_start(out=wd_raw[a][:], in_=wd_rows[a])
-        for q in range(3, 4):
-            nc.sync.dma_start(out=y[q][:], in_=st_rows[:, :, q * QUARTER : (q + 1) * QUARTER])
 
-        v4_codes = keep.tile([P, PASSES, 2 * N], U8, name="v4_codes", align_bytes=64)
-        v4_scales = keep.tile([P, PASSES, N], U8, name="v4_scales", align_bytes=64)
+        def load_x(r):
+            nc.sync.dma_start(out=x_in[r][:], in_=x_rows[r // PACK, r % PACK])
+
+        def load_st(h):
+            for u in range(2):
+                nc.sync.dma_start(out=gate[h, u][:], in_=st_rows[:, 2 * u : 2 * u + 2, h * HALF : (h + 1) * HALF])
+
+        nc.sync.dma_start(out=wgt_sb[:, 0:HALF], in_=wgt[:, 0:HALF])
+        load_x(0)
+        nc.sync.dma_start(out=wgt_sb[:, HALF:J], in_=wgt[:, HALF:J])
+        last = PASSES * PACK - 1
+        for r in range(1, last - 1):
+            load_x(r)
+        nc.sync.dma_start(out=wk_in[0][:], in_=wk_rows[0])
+        load_x(last - 1)
+        nc.sync.dma_start(out=wk_in[1][:], in_=wk_rows[1])
+        nc.sync.dma_start(out=wd_in[0][:], in_=wd_rows[0])
+        load_x(last)
+        load_st(0)
+        nc.sync.dma_start(out=wd_in[1][:], in_=wd_rows[1])
+        load_st(1)
+
+        v4_words = sbuf.tile([P, PASSES, 2 * N], U8, name="v4_words", align_bytes=MX_ALIGN)
+        v4_scales = sbuf.tile([P, PASSES, N], U8, name="v4_scales", align_bytes=MX_ALIGN)
         nc.vector.tensor_copy(
-            out=v4_codes[:].bitcast(U16).rearrange("p a (t m) -> p a m t", t=PACK),
-            in_=v4_raw[:].bitcast(U16).rearrange("p a (m t) -> p a m t", t=PACK),
+            out=v4_words[:].bitcast(U16).rearrange("p a (t m) -> p a t m", t=PACK),
+            in_=v4_words_in[:].bitcast(U16).rearrange("p a (m t) -> p a t m", t=PACK),
         )
         nc.vector.tensor_copy(
-            out=v4_scales[:].rearrange("p a (t m) -> p a m t", t=PACK),
-            in_=v4s_raw[:].rearrange("p a (m t) -> p a m t", t=PACK),
+            out=v4_scales[:].rearrange("p a (t m) -> p a t m", t=PACK),
+            in_=v4_scales_in[:].rearrange("p a (m t) -> p a t m", t=PACK),
         )
+        v4_mx = [
+            [
+                (v4_words[:, a, 2 * P * t : 2 * P * (t + 1)].bitcast(FP4X4), v4_scales[:, a, P * t : P * (t + 1)])
+                for t in range(PACK)
+            ]
+            for a in range(PASSES)
+        ]
 
-        x_codes = {}
-        x_scales = {}
-        for a in range(PASSES):
-            picked = [keep.tile([P, PACK, HALF], F32, name="picked%d%d" % (a, h)) for h in range(2)]
+        def quantise_weight(name, w_in):
+            w_bf = sbuf.tile([P, PACK * N], BF16, name=name + "_bf", align_bytes=MX_ALIGN)
+            nc.scalar.copy(
+                out=w_bf[:].rearrange("p (t m i) -> p m i t", t=PACK, i=PACK),
+                in_=w_in[:].rearrange("p i (m t) -> p m i t", t=PACK),
+            )
+            codes, scales = mx_tiles(name, N)
+            nc.vector.quantize_mx(out=codes[:].bitcast(FP8X4), scales=scales[:], in_=w_bf[:])
+            return [(codes[:, P * t : P * (t + 1)].bitcast(FP8X4), scales[:, P * t : P * (t + 1)]) for t in range(PACK)]
+
+        x_mx = {}
+
+        def pick_and_quantise_x(a, widths, piece):
+            picked = sbuf.tile([P, PACK, J], F32, name="picked%d" % a)
             for i in range(PACK):
-                for h in range(2):
+                for c0 in range(0, J, widths[i]):
+                    c1 = c0 + widths[i]
                     nc.vector.tensor_tensor(
-                        out=picked[h][:, i, :],
-                        in0=planes[a * PACK + i][:].indirect(offsets[:, 32 * h : 32 * (h + 1)]),
-                        in1=wgt_sb[h][:],
+                        out=picked[:, i, c0:c1],
+                        in0=x_in[PACK * a + i][:].indirect(offsets[:, c0 // LIST_ROWS : c1 // LIST_ROWS]),
+                        in1=wgt_sb[:, c0:c1],
                         op=MULT,
                     )
             for h in range(2):
-                x_bf = keep.tile([P, PACK * HALF], BF16, name="x_bf%d%d" % (a, h), align_bytes=64)
-                interleave(nc, ("scalar", "scalar", "scalar", "vector")[2 * a + h], x_bf[:], picked[h][:])
-                x_codes[a, h] = keep.tile([P, HALF], U32, name="x_codes%d%d" % (a, h), align_bytes=64)
-                x_scales[a, h] = keep.tile([P, HALF], U8, name="x_scales%d%d" % (a, h), align_bytes=64)
-                nc.vector.quantize_mx(out=x_codes[a, h][:].bitcast(FP8X4), scales=x_scales[a, h][:], in_=x_bf[:])
-
-        def quantise_weight(name, raw, engines):
-            codes, scales = [], []
-            for u in range(2):
-                w_bf = keep.tile([P, 2 * N], BF16, name="%s_bf%d" % (name, u), align_bytes=64)
-                deal_weight(nc, engines[u], w_bf[:], raw[:], 2 * u, 2 * u + 2)
-                c = keep.tile([P, 2 * P], U32, name="%s_codes%d" % (name, u), align_bytes=64)
-                s = keep.tile([P, 2 * P], U8, name="%s_scales%d" % (name, u), align_bytes=64)
-                nc.vector.quantize_mx(out=c[:].bitcast(FP8X4), scales=s[:], in_=w_bf[:])
-                codes.append(c)
-                scales.append(s)
-            return codes, scales
-
-        def e4m3_pass(bank, w, a, q, u, start, stop):
-            codes, scales = w
-            h = q // 2
-            cols = slice((q % 2) * QUARTER, (q % 2 + 1) * QUARTER)
-            for v in range(2):
-                nc.tensor.matmul_mx(
-                    out=bank[:, v, :],
-                    lhsT=codes[u][:, v * P : (v + 1) * P].bitcast(FP8X4),
-                    lhsT_scale=scales[u][:, v * P : (v + 1) * P],
-                    rhs=x_codes[a, h][:, cols].bitcast(FP8X4),
-                    rhs_scale=x_scales[a, h][:, cols],
-                    start=start and v == 0,
-                    stop=stop and v == 1,
-                )
-
-        def e2m1_pass(bank, a, q, u, start):
-            h = q // 2
-            for v in range(2):
-                t = 2 * u + v
-                for e in range(QUARTER // FP4_N):
-                    c0 = (q % 2) * QUARTER + e * FP4_N
-                    nc.tensor.matmul_mx(
-                        out=bank[:, v, e * FP4_N : (e + 1) * FP4_N],
-                        lhsT=v4_codes[:, a, 2 * P * t : 2 * P * (t + 1)].bitcast(FP4X4),
-                        lhsT_scale=v4_scales[:, a, P * t : P * (t + 1)],
-                        rhs=x_codes[a, h][:, c0 : c0 + FP4_N].bitcast(FP8X4),
-                        rhs_scale=x_scales[a, h][:, c0 : c0 + FP4_N],
-                        start=start and v == 0 and e == 0,
-                        stop=False,
+                x_bf = sbuf.tile([P, PACK * HALF], BF16, name="x_bf%d%d" % (a, h), align_bytes=MX_ALIGN)
+                for c0 in range(0, HALF, piece):
+                    interleave(
+                        nc.scalar.copy,
+                        x_bf[:, PACK * c0 : PACK * (c0 + piece)],
+                        picked[:, :, h * HALF + c0 : h * HALF + c0 + piece],
                     )
+                codes, scales = mx_tiles("x%d%d" % (a, h), HALF)
+                nc.vector.quantize_mx(out=codes[:].bitcast(FP8X4), scales=scales[:], in_=x_bf[:])
+                x_mx[a, h] = (codes[:].bitcast(FP8X4), scales[:])
 
-        wk_q = [quantise_weight("wk%d" % a, wk_raw[a], (("vector", "vector"), ("scalar", "scalar"))[a]) for a in range(PASSES)]
-        ke = {}
-        for q in range(4):
+        def mx_pass(bank, w_slice, a, h, start, stop):
+            nc.tensor.matmul_mx(
+                out=bank[:],
+                lhsT=w_slice[0],
+                lhsT_scale=w_slice[1],
+                rhs=x_mx[a, h][0],
+                rhs_scale=x_mx[a, h][1],
+                start=start,
+                stop=stop,
+            )
+
+        ve = {(0, t): psum.tile([P, HALF], F32, name="ve", tag="bank%d" % (PACK + t)) for t in range(PACK)}
+
+        def first_half_values(w_mx, a, start, stop):
+            for t in range(PACK):
+                mx_pass(ve[0, t], w_mx[t], a, 0, start, stop)
+
+        pick_and_quantise_x(0, (HALF, J, J, J), HALF)
+        first_half_values(v4_mx[0], 0, True, False)
+        wk_mx = [quantise_weight("wk%d" % a, wk_in[a]) for a in range(PASSES)]
+        wd_mx = [quantise_weight("wd0", wd_in[0])]
+        first_half_values(wd_mx[0], 0, False, False)
+        pick_and_quantise_x(1, (J, J, J, QUARTER), QUARTER)
+        wd_mx.append(quantise_weight("wd1", wd_in[1]))
+
+        for h in range(2):
             for u in range(2):
-                ke[q, u] = psum.tile([P, 2, QUARTER], F32, name="ke", tag="bank%d%d" % (q, u))
-        for a in range(PASSES):
-            for q in range(4):
-                for u in range(2):
-                    e4m3_pass(ke[q, u], wk_q[a], a, q, u, a == 0, a == PASSES - 1)
+                for v in range(2):
+                    t = 2 * u + v
+                    ke = psum.tile([P, HALF], F32, name="ke", tag="bank%d" % t)
+                    for a in range(PASSES):
+                        mx_pass(ke, wk_mx[a][t], a, h, a == 0, a == PASSES - 1)
+                    nc.vector.tensor_tensor(out=gate[h, u][:, v, :], in0=ke[:], in1=gate[h, u][:, v, :], op=MULT)
+                nc.scalar.activation(out=gate[h, u][:], in_=gate[h, u][:], func=SIGMOID)
 
-        ve = {}
+        first_half_values(v4_mx[1], 1, False, False)
+        first_half_values(wd_mx[1], 1, False, True)
+        for t in range(PACK):
+            ve[1, t] = psum.tile([P, HALF], F32, name="ve", tag="bank%d" % t)
+            for a in range(PASSES):
+                mx_pass(ve[1, t], v4_mx[a][t], a, 1, a == 0, False)
+            for a in range(PASSES):
+                mx_pass(ve[1, t], wd_mx[a][t], a, 1, False, a == PASSES - 1)
 
-        def gate(q):
-            for u in range(2):
-                rows = y[q][:, 2 * u : 2 * u + 2, :]
-                nc.vector.tensor_tensor(out=rows, in0=ke[q, u][:], in1=rows, op=MULT)
-            nc.scalar.activation(out=y[q][:], in_=y[q][:], func=SIGMOID)
-            for u in range(2):
-                ve[q, u] = psum.tile([P, 2, QUARTER], F32, name="ve", tag="bank%d%d" % (q, u))
-                for a in range(PASSES):
-                    e2m1_pass(ve[q, u], a, q, u, a == 0)
-
-        y_codes = [keep.tile([P, QUARTER], U32, name="y_codes%d" % q, align_bytes=64) for q in range(4)]
-        y_scales = keep.tile([P, J], U8, name="y_scales", align_bytes=64)
+        y_codes, y_scales = mx_tiles("y", J)
         words_out = out_1.rearrange("a p j i -> p (a j i)").bitcast(I32)
+        quarters = J // QUARTER
+        for q in range(quarters):
+            h = q // 2
+            places = slice(q * QUARTER, (q + 1) * QUARTER)
+            in_half = slice((q % 2) * QUARTER, (q % 2 + 1) * QUARTER)
+            y = sbuf.tile([P, PACK, QUARTER], F32, name="y%d" % q)
+            for t in range(PACK):
+                nc.vector.tensor_tensor(
+                    out=y[:, t, :], in0=ve[h, t][:, in_half], in1=gate[h, t // 2][:, t % 2, in_half], op=MULT
+                )
+            nc.sync.dma_start(out=out_rows[:, :, places], in_=y[:])
+            copies = [nc.scalar.copy, nc.vector.tensor_copy] if q == quarters - 1 else [nc.scalar.copy]
+            share = QUARTER // len(copies)
+            y_bf = sbuf.tile([P, PACK * QUARTER], BF16, name="y_bf%d" % q, align_bytes=MX_ALIGN)
+            for n, copy in enumerate(copies):
+                interleave(copy, y_bf[:, PACK * n * share : PACK * (n + 1) * share], y[:, :, n * share : (n + 1) * share])
+            nc.vector.quantize_mx(out=y_codes[:, places].bitcast(FP8X4), scales=y_scales[:, places], in_=y_bf[:])
+            nc.sync.dma_start(out=words_out[:, places], in_=y_codes[:, places].bitcast(I32))
 
-        def finish(q):
-            cols = slice(q * QUARTER, (q + 1) * QUARTER)
-            for u in range(2):
-                rows = y[q][:, 2 * u : 2 * u + 2, :]
-                nc.vector.tensor_tensor(out=rows, in0=ve[q, u][:], in1=rows, op=MULT)
-            nc.sync.dma_start(out=out_rows[:, :, cols], in_=y[q][:])
-            y_bf = keep.tile([P, PACK * QUARTER], BF16, name="y_bf%d" % q, align_bytes=64)
-            interleave(nc, ("scalar", "scalar", "scalar", "scalar")[q], y_bf[:], y[q][:])
-            nc.vector.quantize_mx(out=y_codes[q][:].bitcast(FP8X4), scales=y_scales[:, cols], in_=y_bf[:])
-            nc.sync.dma_start(out=words_out[:, cols], in_=y_codes[q][:].bitcast(I32))
-
-        for q in range(3):
-            gate(q)
-        wd_q = [quantise_weight("wd%d" % a, wd_raw[a], (("vector", "scalar"), ("vector", "scalar"))[a]) for a in range(PASSES)]
-        for a in range(PASSES):
-            for q in range(3):
-                for u in range(2):
-                    e4m3_pass(ve[q, u], wd_q[a], a, q, u, False, a == PASSES - 1)
-        for q in range(3, 4):
-            gate(q)
-            for u in range(2):
-                for a in range(PASSES):
-                    e4m3_pass(ve[q, u], wd_q[a], a, q, u, False, a == PASSES - 1)
-        for q in range(4):
-            finish(q)
-        for q in range(4):
-            queue = nc.sync if q % 2 == 0 else nc.scalar
+        for quad in range(QUADRANTS):
+            queue = nc.sync if quad % 2 == 0 else nc.scalar
             queue.dma_start(
-                out=out_2[0, 4 * q : 4 * q + 4, :].bitcast(I32),
-                in_=y_scales[32 * q : 32 * q + 4, :].bitcast(I32),
+                out=out_2[0, 4 * quad : 4 * quad + 4, :].bitcast(I32),
+                in_=y_scales[32 * quad : 32 * quad + 4, :].bitcast(I32),
             )

@@ -1,6 +1,7 @@
 from contextlib import ExitStack
 
 import concourse.mybir as mybir
+from concourse.masks import make_identity
 
 K, N, T, J = 1024, 512, 2048, 1024
 FLOPS = 3 * 2 * K * N * J
@@ -20,7 +21,9 @@ P = 128
 PACK = 4
 PASSES = K // (P * PACK)
 QUADRANTS = 4
+SCALE_ROWS = 4
 LIST_ROWS = 16
+HEADS = P // LIST_ROWS
 LINE = 4
 HALF = J // 2
 QUARTER = J // 4
@@ -32,6 +35,15 @@ def interleave(copy, out, rows):
         out=out.rearrange("p (b c i) -> p b i c", c=LINE, i=PACK),
         in_=rows.rearrange("p i (b c) -> p b i c", c=LINE),
     )
+
+
+def scale_rows(quad):
+    return slice(SCALE_ROWS * quad, SCALE_ROWS * (quad + 1))
+
+
+def scale_partitions(quad):
+    first = quad * (P // QUADRANTS)
+    return slice(first, first + SCALE_ROWS)
 
 
 def tile_list_dl_sigP_kernel(
@@ -50,25 +62,24 @@ def tile_list_dl_sigP_kernel(
         offsets = sbuf.tile([P, J // LIST_ROWS], U16, name="offsets")
         nc.sync.dma_start(offsets[:], offs)
 
-        v4_words_in = sbuf.tile([P, PASSES, 2 * N], U8, name="v4_words_in")
-        nc.sync.dma_start(out=v4_words_in[:].bitcast(I32), in_=wv4_words.bitcast(I32).rearrange("a p w -> p a w"))
-        v4_scales_in = sbuf.tile([P, PASSES, N], U8, name="v4_scales_in")
-        nc.vector.memset(v4_scales_in[:].bitcast(I32), 0)
-        for quad in range(QUADRANTS):
-            nc.scalar.dma_start(
-                out=v4_scales_in[32 * quad : 32 * quad + 4, :, :].bitcast(I32),
-                in_=wv4_scales[:, 4 * quad : 4 * quad + 4, :].bitcast(I32).rearrange("a r w -> r a w"),
-            )
+        wgt_in = sbuf.tile([P, HALF], F32, name="wgt_in", tag="y1")
+        nc.sync.dma_start(out=wgt_in[0:HEADS, :], in_=wgt.rearrange("(g r) j -> r g j", r=LIST_ROWS)[0][:, HALF:J])
+        wgt_rows = sbuf.tile([P, HALF], F32, name="wgt_rows", tag="y0")
+        nc.gpsimd.memset(wgt_rows[:], 0.0)
+        identity = sbuf.tile([P, P], F32, name="identity")
+        make_identity(nc, identity[:])
 
         warm = sbuf.tile([P, 2], F32, name="warm")
         nc.vector.memset(warm[:, 0:1], 0.0)
         nc.scalar.activation(out=warm[:, 1:2], in_=warm[:, 0:1], func=SIGMOID)
 
-        wgt_sb = sbuf.tile([P, J], F32, name="wgt_sb")
-        x_in = [sbuf.tile([P, T], F32, name="x_in%d" % r) for r in range(PASSES * PACK)]
-        wk_in = [sbuf.tile([P, PACK, N], F32, name="wk_in%d" % a) for a in range(PASSES)]
-        wd_in = [sbuf.tile([P, PACK, N], F32, name="wd_in%d" % a) for a in range(PASSES)]
-        gate = {(h, u): sbuf.tile([P, 2, HALF], F32, name="gate%d%d" % (h, u)) for h in range(2) for u in range(2)}
+        wgt_sb = sbuf.tile([P, J], F32, name="wgt_sb", tag="wgt", align_bytes=MX_ALIGN)
+        v4_words_in = sbuf.tile([P, PASSES, 2 * N], U8, name="v4_words_in")
+        x_in = [sbuf.tile([P, T], F32, name="x_in", tag="x_in%d" % r) for r in range(PASSES * PACK)]
+        wk0_in = sbuf.tile([P, PACK, N], F32, name="wk0_in")
+        wk1_in = [sbuf.tile([P, PACK, N // 2], F32, name="wk1_in%d" % n) for n in range(2)]
+        wd_in = [sbuf.tile([P, PACK, N], F32, name="wd_in", tag="wd_in%d" % a) for a in range(PASSES)]
+        st_sb = {(h, u): sbuf.tile([P, 2, HALF], F32, name="st_sb%d%d" % (h, u)) for h in range(2) for u in range(2)}
         x_rows = xT.rearrange("(a p i) c -> a i p c", p=P, i=PACK)
         wk_rows = wk.rearrange("(a p i) n -> a p i n", p=P, i=PACK)
         wd_rows = wvd.rearrange("(a p i) n -> a p i n", p=P, i=PACK)
@@ -80,25 +91,126 @@ def tile_list_dl_sigP_kernel(
 
         def load_st(h):
             for u in range(2):
-                nc.sync.dma_start(out=gate[h, u][:], in_=st_rows[:, 2 * u : 2 * u + 2, h * HALF : (h + 1) * HALF])
+                nc.sync.dma_start(out=st_sb[h, u][:], in_=st_rows[:, 2 * u : 2 * u + 2, h * HALF : (h + 1) * HALF])
 
         nc.sync.dma_start(out=wgt_sb[:, 0:HALF], in_=wgt[:, 0:HALF])
         load_x(0)
-        nc.sync.dma_start(out=wgt_sb[:, HALF:J], in_=wgt[:, HALF:J])
         last = PASSES * PACK - 1
         for r in range(1, last - 1):
             load_x(r)
-        nc.sync.dma_start(out=wk_in[0][:], in_=wk_rows[0])
+        nc.sync.dma_start(out=wk0_in[:], in_=wk_rows[0])
+        nc.sync.dma_start(out=wk1_in[0][:], in_=wk_rows[1][:, :, 0 : N // 2])
         load_x(last - 1)
-        nc.sync.dma_start(out=wk_in[1][:], in_=wk_rows[1])
-        nc.sync.dma_start(out=wd_in[0][:], in_=wd_rows[0])
+        nc.sync.dma_start(out=wk1_in[1][:], in_=wk_rows[1][:, :, N // 2 : N])
         load_x(last)
+        nc.sync.dma_start(out=v4_words_in[:].bitcast(I32), in_=wv4_words.bitcast(I32).rearrange("a p w -> p a w"))
         load_st(0)
+        nc.sync.dma_start(out=wd_in[0][:], in_=wd_rows[0])
         nc.sync.dma_start(out=wd_in[1][:], in_=wd_rows[1])
         load_st(1)
 
-        v4_words = sbuf.tile([P, PASSES, 2 * N], U8, name="v4_words", align_bytes=MX_ALIGN)
-        v4_scales = sbuf.tile([P, PASSES, N], U8, name="v4_scales", align_bytes=MX_ALIGN)
+        nc.vector.tensor_copy(out=wgt_rows[0:HEADS, :], in_=wgt_in[0:HEADS, :])
+        for q in range(2):
+            turned = psum.tile([P, 2, P], F32, name="turned", tag="bank%d" % q)
+            for b in range(2):
+                c0 = q * QUARTER + b * P
+                nc.tensor.transpose(turned[:, b, :], wgt_rows[:, c0 : c0 + P], identity[:])
+            repeated = sbuf.tile([P, 2, HEADS, LIST_ROWS], F32, name="repeated", tag="y_bf%d" % q, align_bytes=MX_ALIGN)
+            by_head = turned[:, :, 0:HEADS].unsqueeze(3)
+            nc.scalar.copy(out=repeated[:], in_=by_head.to_broadcast([P, 2, HEADS, LIST_ROWS]))
+            back = psum.tile([P, 2, P], F32, name="back", tag="bank%d" % (PACK + q))
+            for b in range(2):
+                nc.tensor.transpose(back[:, b, :], repeated[:, b].rearrange("p g r -> p (g r)"), identity[:])
+            c0 = HALF + q * QUARTER
+            nc.scalar.copy(out=wgt_sb[:, c0 : c0 + QUARTER], in_=back[:].rearrange("p b c -> p (b c)"))
+
+        def deal_weight(name, parts):
+            w_bf = sbuf.tile([P, PACK * N], BF16, name=name + "_bf", align_bytes=MX_ALIGN)
+            share = P // len(parts)
+            for n, (copy, columns) in enumerate(parts):
+                copy(
+                    out=w_bf[:].rearrange("p (t m i) -> p m i t", t=PACK, i=PACK)[:, n * share : (n + 1) * share],
+                    in_=columns.rearrange("p i (m t) -> p m i t", t=PACK),
+                )
+            return w_bf
+
+        def quantise_weight(name, w_bf, scales):
+            codes = sbuf.tile([P, N], U32, name=name + "_codes", align_bytes=MX_ALIGN)
+            nc.vector.quantize_mx(out=codes[:].bitcast(FP8X4), scales=scales, in_=w_bf[:])
+            return [(codes[:, P * t : P * (t + 1)].bitcast(FP8X4), scales[:, P * t : P * (t + 1)]) for t in range(PACK)]
+
+        x_mx = {}
+        picked = [sbuf.tile([P, PACK, J], F32, name="picked%d" % a) for a in range(PASSES)]
+
+        def pick(r, c0, width):
+            nc.vector.tensor_tensor(
+                out=picked[r // PACK][:, r % PACK, c0 : c0 + width],
+                in0=x_in[r][:].indirect(offsets[:, c0 // LIST_ROWS : (c0 + width) // LIST_ROWS]),
+                in1=wgt_sb[:, c0 : c0 + width],
+                op=MULT,
+            )
+
+        def quantise_x(a, h, piece):
+            x_bf = sbuf.tile([P, PACK * HALF], BF16, name="x_bf", tag="x_bf%d%d" % (a, h), align_bytes=MX_ALIGN)
+            for c0 in range(0, HALF, piece):
+                interleave(
+                    nc.scalar.copy,
+                    x_bf[:, PACK * c0 : PACK * (c0 + piece)],
+                    picked[a][:, :, h * HALF + c0 : h * HALF + c0 + piece],
+                )
+            codes, scales = mx_tiles("x%d%d" % (a, h), HALF)
+            nc.vector.quantize_mx(out=codes[:].bitcast(FP8X4), scales=scales[:], in_=x_bf[:])
+            x_mx[a, h] = (codes[:].bitcast(FP8X4), scales[:])
+
+        def mx_pass(bank, w_slice, a, h, start, stop):
+            nc.tensor.matmul_mx(
+                out=bank[:],
+                lhsT=w_slice[0],
+                lhsT_scale=w_slice[1],
+                rhs=x_mx[a, h][0],
+                rhs_scale=x_mx[a, h][1],
+                start=start,
+                stop=stop,
+            )
+
+        def bank(name, h, t):
+            return psum.tile([P, HALF], F32, name=name, tag="bank%d" % (PACK * h + t))
+
+        ke = {(h, t): bank("ke", h, t) for h in range(2) for t in range(PACK)}
+
+        for h in range(2):
+            pick(0, h * HALF, HALF)
+        v4_scales_in = sbuf.tile([P, PASSES, N], U8, name="v4_scales_in", tag="x_in0")
+        nc.gpsimd.memset(v4_scales_in[:].bitcast(I32), 0)
+        for quad in range(QUADRANTS):
+            nc.scalar.dma_start(
+                out=v4_scales_in[scale_partitions(quad), :, :].bitcast(I32),
+                in_=wv4_scales[:, scale_rows(quad), :].bitcast(I32).rearrange("a r w -> r a w"),
+            )
+        for r in range(1, PACK):
+            width = HALF if r == PACK - 1 else J
+            for c0 in range(0, J, width):
+                pick(r, c0, width)
+        for h in range(2):
+            quantise_x(0, h, HALF)
+        wk_scales = sbuf.tile([P, N], U8, name="wk_scales", align_bytes=MX_ALIGN)
+        wk_mx = [
+            quantise_weight("wk0", deal_weight("wk0", [(nc.scalar.copy, wk0_in[:])]), wk_scales[:]),
+            quantise_weight(
+                "wk1", deal_weight("wk1", [(nc.scalar.copy, part[:]) for part in wk1_in]), wk_scales[SCALE_ROWS:P, :]
+            ),
+        ]
+        for h in range(2):
+            for t in range(PACK):
+                mx_pass(ke[h, t], wk_mx[0][t], 0, h, True, False)
+        for r in range(PACK, last):
+            pick(r, 0, J)
+        for q in range(J // QUARTER):
+            pick(last, q * QUARTER, QUARTER)
+        for h in range(2):
+            quantise_x(1, h, QUARTER)
+        v4_words = sbuf.tile([P, PASSES, 2 * N], U8, name="v4_words", tag="x_bf10", align_bytes=MX_ALIGN)
+        v4_scales = sbuf.tile([P, PASSES, N], U8, name="v4_scales", tag="wgt", align_bytes=MX_ALIGN)
         nc.vector.tensor_copy(
             out=v4_words[:].bitcast(U16).rearrange("p a (t m) -> p a t m", t=PACK),
             in_=v4_words_in[:].bitcast(U16).rearrange("p a (m t) -> p a t m", t=PACK),
@@ -115,84 +227,35 @@ def tile_list_dl_sigP_kernel(
             for a in range(PASSES)
         ]
 
-        def quantise_weight(name, w_in):
-            w_bf = sbuf.tile([P, PACK * N], BF16, name=name + "_bf", align_bytes=MX_ALIGN)
-            nc.scalar.copy(
-                out=w_bf[:].rearrange("p (t m i) -> p m i t", t=PACK, i=PACK),
-                in_=w_in[:].rearrange("p i (m t) -> p m i t", t=PACK),
-            )
-            codes, scales = mx_tiles(name, N)
-            nc.vector.quantize_mx(out=codes[:].bitcast(FP8X4), scales=scales[:], in_=w_bf[:])
-            return [(codes[:, P * t : P * (t + 1)].bitcast(FP8X4), scales[:, P * t : P * (t + 1)]) for t in range(PACK)]
-
-        x_mx = {}
-
-        def pick_and_quantise_x(a, widths, piece):
-            picked = sbuf.tile([P, PACK, J], F32, name="picked%d" % a)
-            for i in range(PACK):
-                for c0 in range(0, J, widths[i]):
-                    c1 = c0 + widths[i]
-                    nc.vector.tensor_tensor(
-                        out=picked[:, i, c0:c1],
-                        in0=x_in[PACK * a + i][:].indirect(offsets[:, c0 // LIST_ROWS : c1 // LIST_ROWS]),
-                        in1=wgt_sb[:, c0:c1],
-                        op=MULT,
-                    )
-            for h in range(2):
-                x_bf = sbuf.tile([P, PACK * HALF], BF16, name="x_bf%d%d" % (a, h), align_bytes=MX_ALIGN)
-                for c0 in range(0, HALF, piece):
-                    interleave(
-                        nc.scalar.copy,
-                        x_bf[:, PACK * c0 : PACK * (c0 + piece)],
-                        picked[:, :, h * HALF + c0 : h * HALF + c0 + piece],
-                    )
-                codes, scales = mx_tiles("x%d%d" % (a, h), HALF)
-                nc.vector.quantize_mx(out=codes[:].bitcast(FP8X4), scales=scales[:], in_=x_bf[:])
-                x_mx[a, h] = (codes[:].bitcast(FP8X4), scales[:])
-
-        def mx_pass(bank, w_slice, a, h, start, stop):
-            nc.tensor.matmul_mx(
-                out=bank[:],
-                lhsT=w_slice[0],
-                lhsT_scale=w_slice[1],
-                rhs=x_mx[a, h][0],
-                rhs_scale=x_mx[a, h][1],
-                start=start,
-                stop=stop,
-            )
-
-        ve = {(0, t): psum.tile([P, HALF], F32, name="ve", tag="bank%d" % (PACK + t)) for t in range(PACK)}
-
-        def first_half_values(w_mx, a, start, stop):
-            for t in range(PACK):
-                mx_pass(ve[0, t], w_mx[t], a, 0, start, stop)
-
-        pick_and_quantise_x(0, (HALF, J, J, J), HALF)
-        first_half_values(v4_mx[0], 0, True, False)
-        wk_mx = [quantise_weight("wk%d" % a, wk_in[a]) for a in range(PASSES)]
-        wd_mx = [quantise_weight("wd0", wd_in[0])]
-        first_half_values(wd_mx[0], 0, False, False)
-        pick_and_quantise_x(1, (J, J, J, QUARTER), QUARTER)
-        wd_mx.append(quantise_weight("wd1", wd_in[1]))
-
         for h in range(2):
-            for u in range(2):
-                for v in range(2):
-                    t = 2 * u + v
-                    ke = psum.tile([P, HALF], F32, name="ke", tag="bank%d" % t)
-                    for a in range(PASSES):
-                        mx_pass(ke, wk_mx[a][t], a, h, a == 0, a == PASSES - 1)
-                    nc.vector.tensor_tensor(out=gate[h, u][:, v, :], in0=ke[:], in1=gate[h, u][:, v, :], op=MULT)
-                nc.scalar.activation(out=gate[h, u][:], in_=gate[h, u][:], func=SIGMOID)
+            for t in range(PACK):
+                mx_pass(ke[h, t], wk_mx[1][t], 1, h, False, True)
 
-        first_half_values(v4_mx[1], 1, False, False)
-        first_half_values(wd_mx[1], 1, False, True)
-        for t in range(PACK):
-            ve[1, t] = psum.tile([P, HALF], F32, name="ve", tag="bank%d" % t)
-            for a in range(PASSES):
-                mx_pass(ve[1, t], v4_mx[a][t], a, 1, a == 0, False)
-            for a in range(PASSES):
-                mx_pass(ve[1, t], wd_mx[a][t], a, 1, False, a == PASSES - 1)
+        def multiply_by_ke(h):
+            for t in range(PACK):
+                st_part = st_sb[h, t // 2][:, t % 2, :]
+                nc.vector.tensor_tensor(out=st_part, in0=ke[h, t][:], in1=st_part, op=MULT)
+
+        multiply_by_ke(0)
+        wd_scales = [sbuf.tile([P, N], U8, name="wd_scales%d" % a, align_bytes=MX_ALIGN) for a in range(PASSES)]
+        wd_mx = [quantise_weight("wd0", deal_weight("wd0", [(nc.scalar.copy, wd_in[0][:])]), wd_scales[0][:])]
+        halves = [(nc.scalar.copy, wd_in[1][:, :, 0 : N // 2]), (nc.vector.tensor_copy, wd_in[1][:, :, N // 2 : N])]
+        wd_mx.append(quantise_weight("wd1", deal_weight("wd1", halves), wd_scales[1][:]))
+        multiply_by_ke(1)
+        gate = []
+        for h in range(2):
+            gate.append(sbuf.tile([P, PACK, HALF], F32, name="gate", tag="wd_in%d" % (1 - h)))
+            for u in range(2):
+                nc.scalar.activation(out=gate[h][:, 2 * u : 2 * u + 2, :], in_=st_sb[h, u][:], func=SIGMOID)
+
+        ve = {}
+        for h in range(2):
+            for t in range(PACK):
+                ve[h, t] = bank("ve", h, t)
+                for a in range(PASSES):
+                    mx_pass(ve[h, t], v4_mx[a][t], a, h, a == 0, False)
+                for a in range(PASSES):
+                    mx_pass(ve[h, t], wd_mx[a][t], a, h, False, a == PASSES - 1)
 
         y_codes, y_scales = mx_tiles("y", J)
         words_out = out_1.rearrange("a p j i -> p (a j i)").bitcast(I32)
@@ -201,15 +264,18 @@ def tile_list_dl_sigP_kernel(
             h = q // 2
             places = slice(q * QUARTER, (q + 1) * QUARTER)
             in_half = slice((q % 2) * QUARTER, (q % 2 + 1) * QUARTER)
-            y = sbuf.tile([P, PACK, QUARTER], F32, name="y%d" % q)
+            y = sbuf.tile([P, PACK, QUARTER], F32, name="y", tag="y%d" % q)
             for t in range(PACK):
                 nc.vector.tensor_tensor(
-                    out=y[:, t, :], in0=ve[h, t][:, in_half], in1=gate[h, t // 2][:, t % 2, in_half], op=MULT
+                    out=y[:, t, :], in0=ve[h, t][:, in_half], in1=gate[h][:, t, in_half], op=MULT
                 )
-            nc.sync.dma_start(out=out_rows[:, :, places], in_=y[:])
+                stored = 2 if q == quarters - 1 else PACK
+                if (t + 1) % stored == 0:
+                    slices = slice(t + 1 - stored, t + 1)
+                    nc.sync.dma_start(out=out_rows[:, slices, places], in_=y[:, slices, :])
             copies = [nc.scalar.copy, nc.vector.tensor_copy] if q == quarters - 1 else [nc.scalar.copy]
             share = QUARTER // len(copies)
-            y_bf = sbuf.tile([P, PACK * QUARTER], BF16, name="y_bf%d" % q, align_bytes=MX_ALIGN)
+            y_bf = sbuf.tile([P, PACK * QUARTER], BF16, name="y_bf", tag="y_bf%d" % q, align_bytes=MX_ALIGN)
             for n, copy in enumerate(copies):
                 interleave(copy, y_bf[:, PACK * n * share : PACK * (n + 1) * share], y[:, :, n * share : (n + 1) * share])
             nc.vector.quantize_mx(out=y_codes[:, places].bitcast(FP8X4), scales=y_scales[:, places], in_=y_bf[:])
@@ -218,6 +284,6 @@ def tile_list_dl_sigP_kernel(
         for quad in range(QUADRANTS):
             queue = nc.sync if quad % 2 == 0 else nc.scalar
             queue.dma_start(
-                out=out_2[0, 4 * quad : 4 * quad + 4, :].bitcast(I32),
-                in_=y_scales[32 * quad : 32 * quad + 4, :].bitcast(I32),
+                out=out_2[0, scale_rows(quad), :].bitcast(I32),
+                in_=y_scales[scale_partitions(quad), :].bitcast(I32),
             )

@@ -231,55 +231,89 @@ def tile_list_dl_sigP_kernel(
             for t in range(PACK):
                 mx_pass(ke[h, t], wk_mx[1][t], 1, h, False, True)
 
-        def multiply_by_ke(h):
-            for t in range(PACK):
-                st_part = st_sb[h, t // 2][:, t % 2, :]
+        def multiply_by_ke(h, u):
+            for t in range(2 * u, 2 * u + 2):
+                st_part = st_sb[h, u][:, t % 2, :]
                 nc.vector.tensor_tensor(out=st_part, in0=ke[h, t][:], in1=st_part, op=MULT)
 
-        multiply_by_ke(0)
+        gate = {}
+
+        def sigmoid(h, u, tag):
+            gate[h, u] = sbuf.tile([P, 2, HALF], F32, name="gate", tag=tag)
+            nc.scalar.activation(out=gate[h, u][:], in_=st_sb[h, u][:], func=SIGMOID)
+
+        for u in range(2):
+            multiply_by_ke(0, u)
         wd_scales = [sbuf.tile([P, N], U8, name="wd_scales%d" % a, align_bytes=MX_ALIGN) for a in range(PASSES)]
         wd_mx = [quantise_weight("wd0", deal_weight("wd0", [(nc.scalar.copy, wd_in[0][:])]), wd_scales[0][:])]
         halves = [(nc.scalar.copy, wd_in[1][:, :, 0 : N // 2]), (nc.vector.tensor_copy, wd_in[1][:, :, N // 2 : N])]
         wd_mx.append(quantise_weight("wd1", deal_weight("wd1", halves), wd_scales[1][:]))
-        multiply_by_ke(1)
-        gate = []
-        for h in range(2):
-            gate.append(sbuf.tile([P, PACK, HALF], F32, name="gate", tag="wd_in%d" % (1 - h)))
-            for u in range(2):
-                nc.scalar.activation(out=gate[h][:, 2 * u : 2 * u + 2, :], in_=st_sb[h, u][:], func=SIGMOID)
+        for u in range(2):
+            sigmoid(0, u, "wd_in%d" % (1 - u))
 
-        ve = {}
-        for h in range(2):
-            for t in range(PACK):
-                ve[h, t] = bank("ve", h, t)
-                for a in range(PASSES):
-                    mx_pass(ve[h, t], v4_mx[a][t], a, h, a == 0, False)
-                for a in range(PASSES):
-                    mx_pass(ve[h, t], wd_mx[a][t], a, h, False, a == PASSES - 1)
+        def value_passes(h, t, slot):
+            sums = psum.tile([P, HALF], F32, name="ve", tag="bank%d" % slot)
+            for a in range(PASSES):
+                mx_pass(sums, v4_mx[a][t], a, h, a == 0, False)
+            for a in range(PASSES):
+                mx_pass(sums, wd_mx[a][t], a, h, False, a == PASSES - 1)
+            return sums
 
         y_codes, y_scales = mx_tiles("y", J)
         words_out = out_1.rearrange("a p j i -> p (a j i)").bitcast(I32)
-        quarters = J // QUARTER
-        for q in range(quarters):
-            h = q // 2
+        y = [sbuf.tile([P, PACK, HALF], F32, name="y", tag="x_in%d" % (1 + h)) for h in range(2)]
+
+        def result(h, t, c0, width):
+            nc.vector.tensor_tensor(
+                out=y[h][:, t, c0 : c0 + width],
+                in0=ve[h, t][:, c0 : c0 + width],
+                in1=gate[h, t // 2][:, t % 2, c0 : c0 + width],
+                op=MULT,
+            )
+
+        def store(h, u, c0, width):
+            nc.sync.dma_start(
+                out=out_rows[:, 2 * u : 2 * u + 2, h * HALF + c0 : h * HALF + c0 + width],
+                in_=y[h][:, 2 * u : 2 * u + 2, c0 : c0 + width],
+            )
+
+        def planes(q, copies):
+            h, c0 = q // 2, (q % 2) * QUARTER
             places = slice(q * QUARTER, (q + 1) * QUARTER)
-            in_half = slice((q % 2) * QUARTER, (q % 2 + 1) * QUARTER)
-            y = sbuf.tile([P, PACK, QUARTER], F32, name="y", tag="y%d" % q)
-            for t in range(PACK):
-                nc.vector.tensor_tensor(
-                    out=y[:, t, :], in0=ve[h, t][:, in_half], in1=gate[h][:, t, in_half], op=MULT
-                )
-                stored = 2 if q == quarters - 1 else PACK
-                if (t + 1) % stored == 0:
-                    slices = slice(t + 1 - stored, t + 1)
-                    nc.sync.dma_start(out=out_rows[:, slices, places], in_=y[:, slices, :])
-            copies = [nc.scalar.copy, nc.vector.tensor_copy] if q == quarters - 1 else [nc.scalar.copy]
             share = QUARTER // len(copies)
             y_bf = sbuf.tile([P, PACK * QUARTER], BF16, name="y_bf", tag="y_bf%d" % q, align_bytes=MX_ALIGN)
             for n, copy in enumerate(copies):
-                interleave(copy, y_bf[:, PACK * n * share : PACK * (n + 1) * share], y[:, :, n * share : (n + 1) * share])
+                interleave(
+                    copy,
+                    y_bf[:, PACK * n * share : PACK * (n + 1) * share],
+                    y[h][:, :, c0 + n * share : c0 + (n + 1) * share],
+                )
             nc.vector.quantize_mx(out=y_codes[:, places].bitcast(FP8X4), scales=y_scales[:, places], in_=y_bf[:])
             nc.sync.dma_start(out=words_out[:, places], in_=y_codes[:, places].bitcast(I32))
+
+        ve = {(0, t): value_passes(0, t, t) for t in range(PACK)}
+        multiply_by_ke(1, 0)
+        sigmoid(1, 0, "x_in3")
+        for t in range(2):
+            ve[1, t] = value_passes(1, t, PACK + t)
+        for t in range(PACK):
+            result(0, t, 0, HALF)
+            if t % 2 == 1:
+                store(0, t // 2, 0, HALF)
+        for t in range(2, PACK):
+            ve[1, t] = value_passes(1, t, t - 2)
+        multiply_by_ke(1, 1)
+        planes(0, [nc.scalar.copy])
+        sigmoid(1, 1, "x_in4")
+        planes(1, [nc.scalar.copy])
+        for t in range(2):
+            result(1, t, 0, HALF)
+        store(1, 0, 0, HALF)
+        for q in range(2):
+            for t in range(2, PACK):
+                result(1, t, q * QUARTER, QUARTER)
+            store(1, 1, q * QUARTER, QUARTER)
+            planes(2 + q, [nc.scalar.copy] if q == 0 else [nc.scalar.copy, nc.vector.tensor_copy])
 
         for quad in range(QUADRANTS):
             queue = nc.sync if quad % 2 == 0 else nc.scalar

@@ -15,6 +15,7 @@ U8 = mybir.dt.uint8
 FP8X4 = mybir.dt.float8_e4m3fn_x4
 FP4X4 = mybir.dt.float4_e2m1fn_x4
 MULT = mybir.AluOpType.mult
+ADD = mybir.AluOpType.add
 SIGMOID = mybir.ActivationFunctionType.Sigmoid
 
 P = 128
@@ -69,6 +70,24 @@ def tile_list_dl_sigP_kernel(
         identity = sbuf.tile([P, P], F32, name="identity")
         make_identity(nc, identity[:])
 
+        v4_rows = sbuf.tile([P, PASSES, N], U8, name="v4_rows")
+        v4_scales_in = sbuf.tile([P, PASSES, N], U8, name="v4_scales_in")
+        v4_scales = sbuf.tile([P, PASSES, N], U8, name="v4_scales", align_bytes=MX_ALIGN)
+        nc.vector.memset(v4_scales_in[:].bitcast(I32), 0)
+        for quad in range(QUADRANTS):
+            nc.scalar.dma_start(
+                out=v4_rows[scale_partitions(quad), :, :].bitcast(I32),
+                in_=wv4_scales[:, scale_rows(quad), :].bitcast(I32).rearrange("a r w -> r a w"),
+            )
+            nc.vector.tensor_copy(
+                out=v4_scales_in[scale_partitions(quad), :, :].bitcast(I32),
+                in_=v4_rows[scale_partitions(quad), :, :].bitcast(I32),
+            )
+        nc.vector.tensor_copy(
+            out=v4_scales[:].rearrange("p a (t m) -> p a t m", t=PACK),
+            in_=v4_scales_in[:].rearrange("p a (m t) -> p a t m", t=PACK),
+        )
+
         warm = sbuf.tile([P, 2], F32, name="warm")
         nc.vector.memset(warm[:, 0:1], 0.0)
         nc.scalar.activation(out=warm[:, 1:2], in_=warm[:, 0:1], func=SIGMOID)
@@ -77,7 +96,9 @@ def tile_list_dl_sigP_kernel(
         v4_words_in = sbuf.tile([P, PASSES, 2 * N], U8, name="v4_words_in")
         x_in = [sbuf.tile([P, T], F32, name="x_in", tag="x_in%d" % r) for r in range(PASSES * PACK)]
         wk0_in = sbuf.tile([P, PACK, N], F32, name="wk0_in")
-        wk1_in = [sbuf.tile([P, PACK, N // 2], F32, name="wk1_in%d" % n) for n in range(2)]
+        wk1_in = [
+            sbuf.tile([P, PACK, N // 2], F32, name="wk1_in", tag="wk1_in%d" % n, align_bytes=MX_ALIGN) for n in range(2)
+        ]
         wd_in = [sbuf.tile([P, PACK, N], F32, name="wd_in", tag="wd_in%d" % a) for a in range(PASSES)]
         st_sb = {(h, u): sbuf.tile([P, 2, HALF], F32, name="st_sb%d%d" % (h, u)) for h in range(2) for u in range(2)}
         x_rows = xT.rearrange("(a p i) c -> a i p c", p=P, i=PACK)
@@ -125,7 +146,7 @@ def tile_list_dl_sigP_kernel(
             nc.scalar.copy(out=wgt_sb[:, c0 : c0 + QUARTER], in_=back[:].rearrange("p b c -> p (b c)"))
 
         def deal_weight(name, parts):
-            w_bf = sbuf.tile([P, PACK * N], BF16, name=name + "_bf", align_bytes=MX_ALIGN)
+            w_bf = sbuf.tile([P, PACK * N], BF16, name="w_bf", tag=name + "_bf", align_bytes=MX_ALIGN)
             share = P // len(parts)
             for n, (copy, columns) in enumerate(parts):
                 copy(
@@ -150,16 +171,27 @@ def tile_list_dl_sigP_kernel(
                 op=MULT,
             )
 
-        def quantise_x(a, h, piece):
-            x_bf = sbuf.tile([P, PACK * HALF], BF16, name="x_bf", tag="x_bf%d%d" % (a, h), align_bytes=MX_ALIGN)
-            for c0 in range(0, HALF, piece):
-                interleave(
-                    nc.scalar.copy,
-                    x_bf[:, PACK * c0 : PACK * (c0 + piece)],
-                    picked[a][:, :, h * HALF + c0 : h * HALF + c0 + piece],
-                )
+        x_bf = {}
+
+        def rounded_picks(a, h, tag):
+            x_bf[a, h] = sbuf.tile([P, PACK * HALF], BF16, name="x_bf", tag=tag, align_bytes=MX_ALIGN)
+
+        def round_pair(a, h, u, c0, width):
+            nc.scalar.copy(
+                out=x_bf[a, h][:].rearrange("p (c i) -> p c i", i=PACK)[:, c0 : c0 + width, 2 * u : 2 * u + 2],
+                in_=picked[a][:, 2 * u : 2 * u + 2, h * HALF + c0 : h * HALF + c0 + width].rearrange("p i c -> p c i"),
+            )
+
+        def round_all(a, h, c0, width):
+            interleave(
+                nc.scalar.copy,
+                x_bf[a, h][:, PACK * c0 : PACK * (c0 + width)],
+                picked[a][:, :, h * HALF + c0 : h * HALF + c0 + width],
+            )
+
+        def quantise_x(a, h):
             codes, scales = mx_tiles("x%d%d" % (a, h), HALF)
-            nc.vector.quantize_mx(out=codes[:].bitcast(FP8X4), scales=scales[:], in_=x_bf[:])
+            nc.vector.quantize_mx(out=codes[:].bitcast(FP8X4), scales=scales[:], in_=x_bf[a, h][:])
             x_mx[a, h] = (codes[:].bitcast(FP8X4), scales[:])
 
         def mx_pass(bank, w_slice, a, h, start, stop):
@@ -180,19 +212,17 @@ def tile_list_dl_sigP_kernel(
 
         for h in range(2):
             pick(0, h * HALF, HALF)
-        v4_scales_in = sbuf.tile([P, PASSES, N], U8, name="v4_scales_in", tag="x_in0")
-        nc.gpsimd.memset(v4_scales_in[:].bitcast(I32), 0)
-        for quad in range(QUADRANTS):
-            nc.scalar.dma_start(
-                out=v4_scales_in[scale_partitions(quad), :, :].bitcast(I32),
-                in_=wv4_scales[:, scale_rows(quad), :].bitcast(I32).rearrange("a r w -> r a w"),
-            )
         for r in range(1, PACK):
             width = HALF if r == PACK - 1 else J
             for c0 in range(0, J, width):
                 pick(r, c0, width)
+            if r == 1:
+                for h in range(2):
+                    rounded_picks(0, h, "x_bf0%d" % h)
+                    round_pair(0, h, 0, 0, HALF)
         for h in range(2):
-            quantise_x(0, h, HALF)
+            round_pair(0, h, 1, 0, HALF)
+            quantise_x(0, h)
         wk_scales = sbuf.tile([P, N], U8, name="wk_scales", align_bytes=MX_ALIGN)
         wk_mx = [
             quantise_weight("wk0", deal_weight("wk0", [(nc.scalar.copy, wk0_in[:])]), wk_scales[:]),
@@ -205,19 +235,21 @@ def tile_list_dl_sigP_kernel(
                 mx_pass(ke[h, t], wk_mx[0][t], 0, h, True, False)
         for r in range(PACK, last):
             pick(r, 0, J)
+        rounded_picks(1, 0, "wk1_in1")
+        round_pair(1, 0, 0, 0, HALF)
+        rounded_picks(1, 1, "x_bf11")
         for q in range(J // QUARTER):
             pick(last, q * QUARTER, QUARTER)
-        for h in range(2):
-            quantise_x(1, h, QUARTER)
-        v4_words = sbuf.tile([P, PASSES, 2 * N], U8, name="v4_words", tag="x_bf10", align_bytes=MX_ALIGN)
-        v4_scales = sbuf.tile([P, PASSES, N], U8, name="v4_scales", tag="wgt", align_bytes=MX_ALIGN)
+        for c0 in range(0, HALF, QUARTER):
+            round_pair(1, 0, 1, c0, QUARTER)
+        quantise_x(1, 0)
+        for c0 in range(0, HALF, QUARTER):
+            round_all(1, 1, c0, QUARTER)
+        quantise_x(1, 1)
+        v4_words = sbuf.tile([P, PASSES, 2 * N], U8, name="v4_words", tag="wk1_in1", align_bytes=MX_ALIGN)
         nc.vector.tensor_copy(
             out=v4_words[:].bitcast(U16).rearrange("p a (t m) -> p a t m", t=PACK),
             in_=v4_words_in[:].bitcast(U16).rearrange("p a (m t) -> p a t m", t=PACK),
-        )
-        nc.vector.tensor_copy(
-            out=v4_scales[:].rearrange("p a (t m) -> p a t m", t=PACK),
-            in_=v4_scales_in[:].rearrange("p a (m t) -> p a t m", t=PACK),
         )
         v4_mx = [
             [
@@ -231,25 +263,23 @@ def tile_list_dl_sigP_kernel(
             for t in range(PACK):
                 mx_pass(ke[h, t], wk_mx[1][t], 1, h, False, True)
 
-        def multiply_by_ke(h, u):
-            for t in range(2 * u, 2 * u + 2):
-                st_part = st_sb[h, u][:, t % 2, :]
-                nc.vector.tensor_tensor(out=st_part, in0=ke[h, t][:], in1=st_part, op=MULT)
+        def multiply_by_ke(h, t, out):
+            nc.vector.tensor_tensor(out=out, in0=ke[h, t][:], in1=st_sb[h, t // 2][:, t % 2, :], op=MULT)
 
-        gate = {}
-
-        def sigmoid(h, u, tag):
-            gate[h, u] = sbuf.tile([P, 2, HALF], F32, name="gate", tag=tag)
-            nc.scalar.activation(out=gate[h, u][:], in_=st_sb[h, u][:], func=SIGMOID)
-
-        for u in range(2):
-            multiply_by_ke(0, u)
+        for h, t in [(h, t) for h in range(2) for t in range(PACK)][:-1]:
+            multiply_by_ke(h, t, st_sb[h, t // 2][:, t % 2, :])
         wd_scales = [sbuf.tile([P, N], U8, name="wd_scales%d" % a, align_bytes=MX_ALIGN) for a in range(PASSES)]
-        wd_mx = [quantise_weight("wd0", deal_weight("wd0", [(nc.scalar.copy, wd_in[0][:])]), wd_scales[0][:])]
-        halves = [(nc.scalar.copy, wd_in[1][:, :, 0 : N // 2]), (nc.vector.tensor_copy, wd_in[1][:, :, N // 2 : N])]
-        wd_mx.append(quantise_weight("wd1", deal_weight("wd1", halves), wd_scales[1][:]))
-        for u in range(2):
-            sigmoid(0, u, "wd_in%d" % (1 - u))
+        wd_mx = [
+            quantise_weight("wd%d" % a, deal_weight("wd%d" % a, [(nc.scalar.copy, wd_in[a][:])]), wd_scales[a][:])
+            for a in range(PASSES)
+        ]
+        last_logit = sbuf.tile([P, HALF], F32, name="last_logit", tag="wd1_bf", align_bytes=MX_ALIGN)
+        multiply_by_ke(1, PACK - 1, last_logit[:])
+        gate = [sbuf.tile([P, PACK, HALF], F32, name="gate", tag=tag) for tag in ("wd_in1", "wd_in0")]
+        for h, u in [(0, 0), (0, 1), (1, 0)]:
+            nc.scalar.activation(out=gate[h][:, 2 * u : 2 * u + 2, :], in_=st_sb[h, u][:], func=SIGMOID)
+        nc.scalar.activation(out=gate[1][:, 2, :], in_=st_sb[1, 1][:, 0, :], func=SIGMOID)
+        nc.scalar.activation(out=gate[1][:, 3, :], in_=last_logit[:], func=SIGMOID)
 
         def value_passes(h, t, slot):
             sums = psum.tile([P, HALF], F32, name="ve", tag="bank%d" % slot)
@@ -267,7 +297,7 @@ def tile_list_dl_sigP_kernel(
             nc.vector.tensor_tensor(
                 out=y[h][:, t, c0 : c0 + width],
                 in0=ve[h, t][:, c0 : c0 + width],
-                in1=gate[h, t // 2][:, t % 2, c0 : c0 + width],
+                in1=gate[h][:, t, c0 : c0 + width],
                 op=MULT,
             )
 
@@ -277,35 +307,38 @@ def tile_list_dl_sigP_kernel(
                 in_=y[h][:, 2 * u : 2 * u + 2, c0 : c0 + width],
             )
 
-        def planes(q, copies):
-            h, c0 = q // 2, (q % 2) * QUARTER
-            places = slice(q * QUARTER, (q + 1) * QUARTER)
-            share = QUARTER // len(copies)
-            y_bf = sbuf.tile([P, PACK * QUARTER], BF16, name="y_bf", tag="y_bf%d" % q, align_bytes=MX_ALIGN)
+        def gpsimd_copy(out, in_):
+            nc.gpsimd.tensor_scalar(
+                out=out.rearrange("p b i c -> p b c i"),
+                in0=in_.rearrange("p b i c -> p b c i"),
+                scalar1=1.0,
+                scalar2=0.0,
+                op0=MULT,
+                op1=ADD,
+            )
+
+        def rounded(name, h, c0, width, copies):
+            share = width // len(copies)
+            y_bf = sbuf.tile([P, PACK * width], BF16, name="y_bf", tag=name, align_bytes=MX_ALIGN)
             for n, copy in enumerate(copies):
                 interleave(
                     copy,
                     y_bf[:, PACK * n * share : PACK * (n + 1) * share],
                     y[h][:, :, c0 + n * share : c0 + (n + 1) * share],
                 )
+            return y_bf
+
+        def planes(y_bf, c0, width):
+            places = slice(c0, c0 + width)
             nc.vector.quantize_mx(out=y_codes[:, places].bitcast(FP8X4), scales=y_scales[:, places], in_=y_bf[:])
             nc.sync.dma_start(out=words_out[:, places], in_=y_codes[:, places].bitcast(I32))
 
-        ve = {(0, t): value_passes(0, t, t) for t in range(PACK)}
-        multiply_by_ke(1, 0)
-        sigmoid(1, 0, "x_in3")
-        for t in range(2):
-            ve[1, t] = value_passes(1, t, PACK + t)
+        ve = {(h, t): value_passes(h, t, PACK * h + t) for h in range(2) for t in range(PACK)}
         for t in range(PACK):
             result(0, t, 0, HALF)
             if t % 2 == 1:
                 store(0, t // 2, 0, HALF)
-        for t in range(2, PACK):
-            ve[1, t] = value_passes(1, t, t - 2)
-        multiply_by_ke(1, 1)
-        planes(0, [nc.scalar.copy])
-        sigmoid(1, 1, "x_in4")
-        planes(1, [nc.scalar.copy])
+        pieces = [(rounded("y_bf0", 0, 0, HALF, [nc.scalar.copy, gpsimd_copy]), 0, HALF)]
         for t in range(2):
             result(1, t, 0, HALF)
         store(1, 0, 0, HALF)
@@ -313,7 +346,11 @@ def tile_list_dl_sigP_kernel(
             for t in range(2, PACK):
                 result(1, t, q * QUARTER, QUARTER)
             store(1, 1, q * QUARTER, QUARTER)
-            planes(2 + q, [nc.scalar.copy] if q == 0 else [nc.scalar.copy, nc.vector.tensor_copy])
+        for q in range(2):
+            copies = [nc.scalar.copy, nc.vector.tensor_copy if q else gpsimd_copy]
+            pieces.append((rounded("y_bf%d" % (1 + q), 1, q * QUARTER, QUARTER, copies), HALF + q * QUARTER, QUARTER))
+        for piece in pieces:
+            planes(*piece)
 
         for quad in range(QUADRANTS):
             queue = nc.sync if quad % 2 == 0 else nc.scalar

@@ -63,10 +63,15 @@ def tile_list_dl_sigP_kernel(
         offsets = sbuf.tile([P, J // LIST_ROWS], U16, name="offsets")
         nc.sync.dma_start(offsets[:], offs)
 
-        wgt_in = sbuf.tile([P, HALF], F32, name="wgt_in", tag="y1")
-        nc.sync.dma_start(out=wgt_in[0:HEADS, :], in_=wgt.rearrange("(g r) j -> r g j", r=LIST_ROWS)[0][:, HALF:J])
-        wgt_rows = sbuf.tile([P, HALF], F32, name="wgt_rows", tag="y0")
-        nc.gpsimd.memset(wgt_rows[:], 0.0)
+        first_row = P // QUADRANTS - HEADS
+        wgt_rows = sbuf.tile([P, J - QUARTER], F32, name="wgt_rows")
+        nc.sync.dma_start(
+            out=wgt_rows[first_row : first_row + HEADS, :],
+            in_=wgt.rearrange("(g r) j -> r g j", r=LIST_ROWS)[0][:, QUARTER:J],
+        )
+        nc.vector.memset(wgt_rows[0:first_row, :], 0.0)
+        nc.vector.memset(wgt_rows[P // 4 : P // 2, :], 0.0)
+        nc.gpsimd.memset(wgt_rows[P // 2 : P, :], 0.0)
         identity = sbuf.tile([P, P], F32, name="identity")
         make_identity(nc, identity[:])
 
@@ -114,7 +119,7 @@ def tile_list_dl_sigP_kernel(
             for u in range(2):
                 nc.sync.dma_start(out=st_sb[h, u][:], in_=st_rows[:, 2 * u : 2 * u + 2, h * HALF : (h + 1) * HALF])
 
-        nc.sync.dma_start(out=wgt_sb[:, 0:HALF], in_=wgt[:, 0:HALF])
+        nc.sync.dma_start(out=wgt_sb[:, 0:QUARTER], in_=wgt[:, 0:QUARTER])
         load_x(0)
         last = PASSES * PACK - 1
         for r in range(1, last - 1):
@@ -130,19 +135,18 @@ def tile_list_dl_sigP_kernel(
         nc.sync.dma_start(out=wd_in[1][:], in_=wd_rows[1])
         load_st(1)
 
-        nc.vector.tensor_copy(out=wgt_rows[0:HEADS, :], in_=wgt_in[0:HEADS, :])
-        for q in range(2):
+        for q in range(J // QUARTER - 1):
             turned = psum.tile([P, 2, P], F32, name="turned", tag="bank%d" % q)
             for b in range(2):
                 c0 = q * QUARTER + b * P
                 nc.tensor.transpose(turned[:, b, :], wgt_rows[:, c0 : c0 + P], identity[:])
             repeated = sbuf.tile([P, 2, HEADS, LIST_ROWS], F32, name="repeated", tag="y_bf%d" % q, align_bytes=MX_ALIGN)
-            by_head = turned[:, :, 0:HEADS].unsqueeze(3)
+            by_head = turned[:, :, first_row : first_row + HEADS].unsqueeze(3)
             nc.scalar.copy(out=repeated[:], in_=by_head.to_broadcast([P, 2, HEADS, LIST_ROWS]))
             back = psum.tile([P, 2, P], F32, name="back", tag="bank%d" % (PACK + q))
             for b in range(2):
                 nc.tensor.transpose(back[:, b, :], repeated[:, b].rearrange("p g r -> p (g r)"), identity[:])
-            c0 = HALF + q * QUARTER
+            c0 = (q + 1) * QUARTER
             nc.scalar.copy(out=wgt_sb[:, c0 : c0 + QUARTER], in_=back[:].rearrange("p b c -> p (b c)"))
 
         def deal_weight(name, parts):
@@ -210,8 +214,8 @@ def tile_list_dl_sigP_kernel(
 
         ke = {(h, t): bank("ke", h, t) for h in range(2) for t in range(PACK)}
 
-        for h in range(2):
-            pick(0, h * HALF, HALF)
+        for c0, width in [(0, QUARTER), (QUARTER, QUARTER), (HALF, HALF)]:
+            pick(0, c0, width)
         for r in range(1, PACK):
             width = HALF if r == PACK - 1 else J
             for c0 in range(0, J, width):
@@ -238,13 +242,12 @@ def tile_list_dl_sigP_kernel(
         rounded_picks(1, 0, "wk1_in1")
         round_pair(1, 0, 0, 0, HALF)
         rounded_picks(1, 1, "x_bf11")
-        for q in range(J // QUARTER):
-            pick(last, q * QUARTER, QUARTER)
+        for c0, width in [(0, QUARTER), (QUARTER, QUARTER), (HALF, HALF)]:
+            pick(last, c0, width)
         for c0 in range(0, HALF, QUARTER):
             round_pair(1, 0, 1, c0, QUARTER)
         quantise_x(1, 0)
-        for c0 in range(0, HALF, QUARTER):
-            round_all(1, 1, c0, QUARTER)
+        round_all(1, 1, 0, HALF)
         quantise_x(1, 1)
         v4_words = sbuf.tile([P, PASSES, 2 * N], U8, name="v4_words", tag="wk1_in1", align_bytes=MX_ALIGN)
         nc.vector.tensor_copy(
@@ -312,7 +315,7 @@ def tile_list_dl_sigP_kernel(
                 out=out.rearrange("p b i c -> p b c i"),
                 in0=in_.rearrange("p b i c -> p b c i"),
                 scalar1=1.0,
-                scalar2=0.0,
+                scalar2=-0.0,
                 op0=MULT,
                 op1=ADD,
             )

@@ -304,11 +304,8 @@ def tile_list_dl_sigP_kernel(
                 op=MULT,
             )
 
-        def store(h, u, c0, width):
-            nc.sync.dma_start(
-                out=out_rows[:, 2 * u : 2 * u + 2, h * HALF + c0 : h * HALF + c0 + width],
-                in_=y[h][:, 2 * u : 2 * u + 2, c0 : c0 + width],
-            )
+        def store(h, slices):
+            nc.sync.dma_start(out=out_rows[:, slices, h * HALF : (h + 1) * HALF], in_=y[h][:, slices, :])
 
         def gpsimd_copy(out, in_):
             nc.gpsimd.tensor_scalar(
@@ -337,21 +334,18 @@ def tile_list_dl_sigP_kernel(
             nc.sync.dma_start(out=words_out[:, places], in_=y_codes[:, places].bitcast(I32))
 
         ve = {(h, t): value_passes(h, t, PACK * h + t) for h in range(2) for t in range(PACK)}
-        for t in range(PACK):
-            result(0, t, 0, HALF)
-            if t % 2 == 1:
-                store(0, t // 2, 0, HALF)
+        for h in range(2):
+            for t in range(PACK):
+                width = QUARTER if (h, t) == (1, PACK - 1) else HALF
+                for c0 in range(0, HALF, width):
+                    result(h, t, c0, width)
+                if (h, t // 2) == (1, 1):
+                    store(h, slice(t, t + 1))
+                elif t % 2 == 1:
+                    store(h, slice(t - 1, t + 1))
         pieces = [(rounded("y_bf0", 0, 0, HALF, [nc.scalar.copy, gpsimd_copy]), 0, HALF)]
-        for t in range(2):
-            result(1, t, 0, HALF)
-        store(1, 0, 0, HALF)
-        for q in range(2):
-            for t in range(2, PACK):
-                result(1, t, q * QUARTER, QUARTER)
-            store(1, 1, q * QUARTER, QUARTER)
-        for q in range(2):
-            copies = [nc.scalar.copy, nc.vector.tensor_copy if q else gpsimd_copy]
-            pieces.append((rounded("y_bf%d" % (1 + q), 1, q * QUARTER, QUARTER, copies), HALF + q * QUARTER, QUARTER))
+        for q, copy in enumerate((nc.scalar.copy, nc.vector.tensor_copy)):
+            pieces.append((rounded("y_bf%d" % (1 + q), 1, q * QUARTER, QUARTER, [copy]), HALF + q * QUARTER, QUARTER))
         for piece in pieces:
             planes(*piece)
 

@@ -63,15 +63,14 @@ def tile_list_dl_sigP_kernel(
         offsets = sbuf.tile([P, J // LIST_ROWS], U16, name="offsets")
         nc.sync.dma_start(offsets[:], offs)
 
-        first_row = P // QUADRANTS - HEADS
-        wgt_rows = sbuf.tile([P, J - QUARTER], F32, name="wgt_rows")
+        runs = HALF // P
+        wgt_rows = sbuf.tile([P, P], F32, name="wgt_rows")
         nc.sync.dma_start(
-            out=wgt_rows[first_row : first_row + HEADS, :],
-            in_=wgt.rearrange("(g r) j -> r g j", r=LIST_ROWS)[0][:, QUARTER:J],
+            out=wgt_rows[0 : runs * HEADS, :],
+            in_=wgt[:, HALF:J].rearrange("(g r) (s c) -> r g s c", r=LIST_ROWS, c=P)[0],
         )
-        nc.vector.memset(wgt_rows[0:first_row, :], 0.0)
         nc.vector.memset(wgt_rows[P // 4 : P // 2, :], 0.0)
-        nc.gpsimd.memset(wgt_rows[P // 2 : P, :], 0.0)
+        nc.vector.memset(wgt_rows[P // 2 : P, :], 0.0)
         identity = sbuf.tile([P, P], F32, name="identity")
         make_identity(nc, identity[:])
 
@@ -119,7 +118,7 @@ def tile_list_dl_sigP_kernel(
             for u in range(2):
                 nc.sync.dma_start(out=st_sb[h, u][:], in_=st_rows[:, 2 * u : 2 * u + 2, h * HALF : (h + 1) * HALF])
 
-        nc.sync.dma_start(out=wgt_sb[:, 0:QUARTER], in_=wgt[:, 0:QUARTER])
+        nc.sync.dma_start(out=wgt_sb[:, 0:HALF], in_=wgt[:, 0:HALF])
         load_x(0)
         last = PASSES * PACK - 1
         for r in range(1, last - 1):
@@ -135,19 +134,15 @@ def tile_list_dl_sigP_kernel(
         nc.sync.dma_start(out=wd_in[1][:], in_=wd_rows[1])
         load_st(1)
 
-        for q in range(J // QUARTER - 1):
-            turned = psum.tile([P, 2, P], F32, name="turned", tag="bank%d" % q)
-            for b in range(2):
-                c0 = q * QUARTER + b * P
-                nc.tensor.transpose(turned[:, b, :], wgt_rows[:, c0 : c0 + P], identity[:])
-            repeated = sbuf.tile([P, 2, HEADS, LIST_ROWS], F32, name="repeated", tag="y_bf%d" % q, align_bytes=MX_ALIGN)
-            by_head = turned[:, :, first_row : first_row + HEADS].unsqueeze(3)
-            nc.scalar.copy(out=repeated[:], in_=by_head.to_broadcast([P, 2, HEADS, LIST_ROWS]))
-            back = psum.tile([P, 2, P], F32, name="back", tag="bank%d" % (PACK + q))
-            for b in range(2):
-                nc.tensor.transpose(back[:, b, :], repeated[:, b].rearrange("p g r -> p (g r)"), identity[:])
-            c0 = (q + 1) * QUARTER
-            nc.scalar.copy(out=wgt_sb[:, c0 : c0 + QUARTER], in_=back[:].rearrange("p b c -> p (b c)"))
+        turned = psum.tile([P, P], F32, name="turned", tag="bank0")
+        nc.tensor.transpose(turned[:], wgt_rows[:], identity[:])
+        repeated = sbuf.tile([P, runs, HEADS, LIST_ROWS], F32, name="repeated", tag="y_bf0", align_bytes=MX_ALIGN)
+        by_head = turned[:, 0 : runs * HEADS].rearrange("p (g s) -> p s g", g=HEADS).unsqueeze(3)
+        nc.scalar.copy(out=repeated[:], in_=by_head.to_broadcast([P, runs, HEADS, LIST_ROWS]))
+        back = psum.tile([P, runs, P], F32, name="back", tag="bank1")
+        for s in range(runs):
+            nc.tensor.transpose(back[:, s, :], repeated[:, s].rearrange("p g r -> p (g r)"), identity[:])
+        nc.scalar.copy(out=wgt_sb[:, HALF:J], in_=back[:].rearrange("p s c -> p (s c)"))
 
         def deal_weight(name, parts):
             w_bf = sbuf.tile([P, PACK * N], BF16, name="w_bf", tag=name + "_bf", align_bytes=MX_ALIGN)
@@ -214,8 +209,8 @@ def tile_list_dl_sigP_kernel(
 
         ke = {(h, t): bank("ke", h, t) for h in range(2) for t in range(PACK)}
 
-        for c0, width in [(0, QUARTER), (QUARTER, QUARTER), (HALF, HALF)]:
-            pick(0, c0, width)
+        for c0 in range(0, J, HALF):
+            pick(0, c0, HALF)
         for r in range(1, PACK):
             width = HALF if r == PACK - 1 else J
             for c0 in range(0, J, width):

@@ -98,7 +98,7 @@ def tile_list_dl_sigP_kernel(
 
         wgt_sb = sbuf.tile([P, J], F32, name="wgt_sb", tag="wgt", align_bytes=MX_ALIGN)
         v4_words_in = sbuf.tile([P, PASSES, 2 * N], U8, name="v4_words_in")
-        x_in = [sbuf.tile([P, T], F32, name="x_in", tag="x_in%d" % r) for r in range(PASSES * PACK)]
+        x_in = [sbuf.tile([P, T], F32, name="x_in", tag="x_in%d" % r, align_bytes=MX_ALIGN) for r in range(PASSES * PACK)]
         wk0_in = sbuf.tile([P, PACK, N], F32, name="wk0_in")
         wk1_in = [
             sbuf.tile([P, PACK, N // 2], F32, name="wk1_in", tag="wk1_in%d" % n, align_bytes=MX_ALIGN) for n in range(2)
@@ -162,9 +162,9 @@ def tile_list_dl_sigP_kernel(
         x_mx = {}
         picked = [sbuf.tile([P, PACK, J], F32, name="picked%d" % a) for a in range(PASSES)]
 
-        def pick(r, c0, width):
+        def pick(r, c0, width, out=None):
             nc.vector.tensor_tensor(
-                out=picked[r // PACK][:, r % PACK, c0 : c0 + width],
+                out=picked[r // PACK][:, r % PACK, c0 : c0 + width] if out is None else out,
                 in0=x_in[r][:].indirect(offsets[:, c0 // LIST_ROWS : (c0 + width) // LIST_ROWS]),
                 in1=wgt_sb[:, c0 : c0 + width],
                 op=MULT,
@@ -175,10 +175,12 @@ def tile_list_dl_sigP_kernel(
         def rounded_picks(a, h, tag):
             x_bf[a, h] = sbuf.tile([P, PACK * HALF], BF16, name="x_bf", tag=tag, align_bytes=MX_ALIGN)
 
-        def round_pair(a, h, u, c0, width):
+        def round_pair(a, h, u, c0, width, pair=None):
+            if pair is None:
+                pair = picked[a][:, 2 * u : 2 * u + 2, h * HALF + c0 : h * HALF + c0 + width]
             nc.scalar.copy(
                 out=x_bf[a, h][:].rearrange("p (c i) -> p c i", i=PACK)[:, c0 : c0 + width, 2 * u : 2 * u + 2],
-                in_=picked[a][:, 2 * u : 2 * u + 2, h * HALF + c0 : h * HALF + c0 + width].rearrange("p i c -> p c i"),
+                in_=pair.rearrange("p i c -> p c i"),
             )
 
         def round_all(a, h, c0, width):
@@ -232,19 +234,23 @@ def tile_list_dl_sigP_kernel(
         for h in range(2):
             for t in range(PACK):
                 mx_pass(ke[h, t], wk_mx[0][t], 0, h, True, False)
-        for r in range(PACK, last):
+        for r in range(PACK, last - 1):
             pick(r, 0, J)
+        last_pair = sbuf.tile([P, 2, HALF], F32, name="last_pair", tag="x_in0", align_bytes=MX_ALIGN)
+        pick(last - 1, 0, HALF, last_pair[:, 0, :])
+        pick(last - 1, HALF, HALF)
         rounded_picks(1, 0, "wk1_in1")
         round_pair(1, 0, 0, 0, HALF)
         rounded_picks(1, 1, "x_bf11")
-        for c0, width in [(0, QUARTER), (QUARTER, QUARTER), (HALF, HALF)]:
-            pick(last, c0, width)
         for c0 in range(0, HALF, QUARTER):
-            round_pair(1, 0, 1, c0, QUARTER)
+            pick(last, c0, QUARTER, last_pair[:, 1, c0 : c0 + QUARTER])
+        pick(last, HALF, HALF)
+        for c0 in range(0, HALF, QUARTER):
+            round_pair(1, 0, 1, c0, QUARTER, last_pair[:, :, c0 : c0 + QUARTER])
         quantise_x(1, 0)
         round_all(1, 1, 0, HALF)
         quantise_x(1, 1)
-        v4_words = sbuf.tile([P, PASSES, 2 * N], U8, name="v4_words", tag="wk1_in1", align_bytes=MX_ALIGN)
+        v4_words = sbuf.tile([P, PASSES, 2 * N], U8, name="v4_words", tag="x_in0", align_bytes=MX_ALIGN)
         nc.vector.tensor_copy(
             out=v4_words[:].bitcast(U16).rearrange("p a (t m) -> p a t m", t=PACK),
             in_=v4_words_in[:].bitcast(U16).rearrange("p a (m t) -> p a t m", t=PACK),
@@ -271,13 +277,13 @@ def tile_list_dl_sigP_kernel(
             quantise_weight("wd%d" % a, deal_weight("wd%d" % a, [(nc.scalar.copy, wd_in[a][:])]), wd_scales[a][:])
             for a in range(PASSES)
         ]
-        last_logit = sbuf.tile([P, HALF], F32, name="last_logit", tag="wd1_bf", align_bytes=MX_ALIGN)
-        multiply_by_ke(1, PACK - 1, last_logit[:])
-        gate = [sbuf.tile([P, PACK, HALF], F32, name="gate", tag=tag) for tag in ("wd_in1", "wd_in0")]
+        gate = [sbuf.tile([P, PACK + 1 - h, HALF], F32, name="gate", tag="wd_in%d" % (1 - h)) for h in range(2)]
+        last_logit = gate[0][:, PACK, :]
+        multiply_by_ke(1, PACK - 1, last_logit)
         for h, u in [(0, 0), (0, 1), (1, 0)]:
             nc.scalar.activation(out=gate[h][:, 2 * u : 2 * u + 2, :], in_=st_sb[h, u][:], func=SIGMOID)
         nc.scalar.activation(out=gate[1][:, 2, :], in_=st_sb[1, 1][:, 0, :], func=SIGMOID)
-        nc.scalar.activation(out=gate[1][:, 3, :], in_=last_logit[:], func=SIGMOID)
+        nc.scalar.activation(out=gate[1][:, 3, :], in_=last_logit, func=SIGMOID)
 
         def value_passes(h, t, slot):
             sums = psum.tile([P, HALF], F32, name="ve", tag="bank%d" % slot)
@@ -289,7 +295,7 @@ def tile_list_dl_sigP_kernel(
 
         y_codes, y_scales = mx_tiles("y", J)
         words_out = out_1.rearrange("a p j i -> p (a j i)").bitcast(I32)
-        y = [sbuf.tile([P, PACK, HALF], F32, name="y", tag="x_in%d" % (1 + h)) for h in range(2)]
+        y = [sbuf.tile([P, PACK, HALF], F32, name="y", tag="x_in%d" % (1 + h), align_bytes=MX_ALIGN) for h in range(2)]
 
         def result(h, t, c0, width):
             nc.vector.tensor_tensor(

@@ -28,6 +28,7 @@ HEADS = P // LIST_ROWS
 LINE = 4
 HALF = J // 2
 QUARTER = J // 4
+VECTOR_SHARE = 96
 MX_ALIGN = 64
 
 
@@ -53,30 +54,29 @@ def tile_list_dl_sigP_kernel(
     nc = tc.nc
     with ExitStack() as ctx:
         sbuf = ctx.enter_context(tc.tile_pool(name="sbuf", bufs=1))
+        shared = ctx.enter_context(tc.tile_pool(name="shared", bufs=1))
         psum = ctx.enter_context(tc.psum_pool(name="psum", bufs=1))
 
-        def mx_tiles(name, width):
-            codes = sbuf.tile([P, width], U32, name=name + "_codes", align_bytes=MX_ALIGN)
-            scales = sbuf.tile([P, width], U8, name=name + "_scales", align_bytes=MX_ALIGN)
-            return codes, scales
+        def tile(name, shape, dtype, tag=None):
+            return sbuf.tile([P] + shape, dtype, name=name, tag=tag or name, align_bytes=MX_ALIGN)
 
         offsets = sbuf.tile([P, J // LIST_ROWS], U16, name="offsets")
         nc.sync.dma_start(offsets[:], offs)
 
         runs = HALF // P
-        wgt_rows = sbuf.tile([P, P], F32, name="wgt_rows")
+        wgt_rows = tile("wgt_rows", [P], F32)
         nc.sync.dma_start(
             out=wgt_rows[0 : runs * HEADS, :],
             in_=wgt[:, HALF:J].rearrange("(g r) (s c) -> r g s c", r=LIST_ROWS, c=P)[0],
         )
         nc.vector.memset(wgt_rows[P // 4 : P // 2, :], 0.0)
         nc.vector.memset(wgt_rows[P // 2 : P, :], 0.0)
-        identity = sbuf.tile([P, P], F32, name="identity")
+        identity = tile("identity", [P], F32)
         make_identity(nc, identity[:])
 
-        v4_rows = sbuf.tile([P, PASSES, N], U8, name="v4_rows")
-        v4_scales_in = sbuf.tile([P, PASSES, N], U8, name="v4_scales_in")
-        v4_scales = sbuf.tile([P, PASSES, N], U8, name="v4_scales", align_bytes=MX_ALIGN)
+        v4_rows = tile("v4_rows", [PASSES, N], U8)
+        v4_scales_in = tile("v4_scales_in", [PASSES, N], U8)
+        v4_scales = tile("v4_scales", [PASSES, N], U8)
         nc.vector.memset(v4_scales_in[:].bitcast(I32), 0)
         for quad in range(QUADRANTS):
             nc.scalar.dma_start(
@@ -92,51 +92,49 @@ def tile_list_dl_sigP_kernel(
             in_=v4_scales_in[:].rearrange("p a (m t) -> p a t m", t=PACK),
         )
 
-        warm = sbuf.tile([P, 2], F32, name="warm")
+        warm = tile("warm", [2], F32)
         nc.vector.memset(warm[:, 0:1], 0.0)
         nc.scalar.activation(out=warm[:, 1:2], in_=warm[:, 0:1], func=SIGMOID)
 
-        wgt_sb = sbuf.tile([P, J], F32, name="wgt_sb", tag="wgt", align_bytes=MX_ALIGN)
-        v4_words_in = sbuf.tile([P, PASSES, 2 * N], U8, name="v4_words_in")
-        x_in = [sbuf.tile([P, T], F32, name="x_in", tag="x_in%d" % r, align_bytes=MX_ALIGN) for r in range(PASSES * PACK)]
-        wk0_in = sbuf.tile([P, PACK, N], F32, name="wk0_in")
-        wk1_in = [
-            sbuf.tile([P, PACK, N // 2], F32, name="wk1_in", tag="wk1_in%d" % n, align_bytes=MX_ALIGN) for n in range(2)
+        windows = PASSES * PACK
+        wgt_sb = tile("wgt_sb", [J], F32)
+        v4_words_in = tile("v4_words_in", [PASSES, 2 * N], U8)
+        x_in = [tile("x_in%d" % r, [T], F32) for r in range(windows)]
+        wk_in = [
+            shared.tile([P, PACK, N], F32, name="wk_in0", offset=0, align_bytes=MX_ALIGN),
+            shared.tile([P, PACK, N], F32, name="wk_in1", offset=4 * PACK * N, align_bytes=MX_ALIGN),
         ]
-        wd_in = [sbuf.tile([P, PACK, N], F32, name="wd_in", tag="wd_in%d" % a) for a in range(PASSES)]
-        st_sb = {(h, u): sbuf.tile([P, 2, HALF], F32, name="st_sb%d%d" % (h, u)) for h in range(2) for u in range(2)}
+        wd_in = [tile("wd_in%d" % a, [PACK, N], F32) for a in range(PASSES)]
+        st_sb = {(h, u): tile("st_sb%d%d" % (h, u), [2, HALF], F32) for h in range(2) for u in range(2)}
         x_rows = xT.rearrange("(a p i) c -> a i p c", p=P, i=PACK)
         wk_rows = wk.rearrange("(a p i) n -> a p i n", p=P, i=PACK)
         wd_rows = wvd.rearrange("(a p i) n -> a p i n", p=P, i=PACK)
         st_rows = st.rearrange("(p t) j -> p t j", t=PACK)
         out_rows = out_0.rearrange("(p t) j -> p t j", t=PACK)
 
-        def load_x(r):
-            nc.sync.dma_start(out=x_in[r][:], in_=x_rows[r // PACK, r % PACK])
+        def load_x(first, end):
+            for r in range(first, end):
+                nc.sync.dma_start(out=x_in[r][:], in_=x_rows[r // PACK, r % PACK])
 
         def load_st(h):
             for u in range(2):
                 nc.sync.dma_start(out=st_sb[h, u][:], in_=st_rows[:, 2 * u : 2 * u + 2, h * HALF : (h + 1) * HALF])
 
         nc.sync.dma_start(out=wgt_sb[:, 0:HALF], in_=wgt[:, 0:HALF])
-        load_x(0)
-        last = PASSES * PACK - 1
-        for r in range(1, last - 1):
-            load_x(r)
-        nc.sync.dma_start(out=wk0_in[:], in_=wk_rows[0])
-        nc.sync.dma_start(out=wk1_in[0][:], in_=wk_rows[1][:, :, 0 : N // 2])
-        load_x(last - 1)
-        nc.sync.dma_start(out=wk1_in[1][:], in_=wk_rows[1][:, :, N // 2 : N])
-        load_x(last)
+        load_x(0, PACK + 1)
         nc.sync.dma_start(out=v4_words_in[:].bitcast(I32), in_=wv4_words.bitcast(I32).rearrange("a p w -> p a w"))
-        load_st(0)
+        load_x(PACK + 1, windows - 2)
+        nc.sync.dma_start(out=wk_in[0][:], in_=wk_rows[0])
+        load_x(windows - 2, windows)
+        nc.sync.dma_start(out=wk_in[1][:], in_=wk_rows[1])
         nc.sync.dma_start(out=wd_in[0][:], in_=wd_rows[0])
+        load_st(0)
         nc.sync.dma_start(out=wd_in[1][:], in_=wd_rows[1])
         load_st(1)
 
         turned = psum.tile([P, P], F32, name="turned", tag="bank0")
         nc.tensor.transpose(turned[:], wgt_rows[:], identity[:])
-        repeated = sbuf.tile([P, runs, HEADS, LIST_ROWS], F32, name="repeated", tag="y_bf0", align_bytes=MX_ALIGN)
+        repeated = tile("repeated", [runs, HEADS, LIST_ROWS], F32)
         by_head = turned[:, 0 : runs * HEADS].rearrange("p (g s) -> p s g", g=HEADS).unsqueeze(3)
         nc.scalar.copy(out=repeated[:], in_=by_head.to_broadcast([P, runs, HEADS, LIST_ROWS]))
         back = psum.tile([P, runs, P], F32, name="back", tag="bank1")
@@ -144,55 +142,47 @@ def tile_list_dl_sigP_kernel(
             nc.tensor.transpose(back[:, s, :], repeated[:, s].rearrange("p g r -> p (g r)"), identity[:])
         nc.scalar.copy(out=wgt_sb[:, HALF:J], in_=back[:].rearrange("p s c -> p (s c)"))
 
-        def deal_weight(name, parts):
-            w_bf = sbuf.tile([P, PACK * N], BF16, name="w_bf", tag=name + "_bf", align_bytes=MX_ALIGN)
-            share = P // len(parts)
-            for n, (copy, columns) in enumerate(parts):
-                copy(
-                    out=w_bf[:].rearrange("p (t m i) -> p m i t", t=PACK, i=PACK)[:, n * share : (n + 1) * share],
-                    in_=columns.rearrange("p i (m t) -> p m i t", t=PACK),
-                )
-            return w_bf
+        def deal(copy, w_bf, w_in, m0, m1):
+            copy(
+                out=w_bf[:].rearrange("p (t m i) -> p m i t", t=PACK, i=PACK)[:, m0:m1],
+                in_=w_in[:].rearrange("p i (m t) -> p m i t", t=PACK)[:, m0:m1],
+            )
 
-        def quantise_weight(name, w_bf, scales):
-            codes = sbuf.tile([P, N], U32, name=name + "_codes", align_bytes=MX_ALIGN)
-            nc.vector.quantize_mx(out=codes[:].bitcast(FP8X4), scales=scales, in_=w_bf[:])
+        def quantise(name, values, tag=None):
+            width = values.shape[1] // PACK
+            codes = tile(name + "_codes", [width], U32, tag)
+            scales = tile(name + "_scales", [width], U8)[:]
+            nc.vector.quantize_mx(out=codes[:].bitcast(FP8X4), scales=scales, in_=values)
+            return codes, scales
+
+        def slices(codes, scales):
             return [(codes[:, P * t : P * (t + 1)].bitcast(FP8X4), scales[:, P * t : P * (t + 1)]) for t in range(PACK)]
 
-        x_mx = {}
-        picked = [sbuf.tile([P, PACK, J], F32, name="picked%d" % a) for a in range(PASSES)]
+        picked = [tile("picked%d" % pair, [2, J], F32) for pair in range(windows // 2)]
 
-        def pick(r, c0, width, out=None):
+        def pick(r, c0, width):
             nc.vector.tensor_tensor(
-                out=picked[r // PACK][:, r % PACK, c0 : c0 + width] if out is None else out,
+                out=picked[r // 2][:, r % 2, c0 : c0 + width],
                 in0=x_in[r][:].indirect(offsets[:, c0 // LIST_ROWS : (c0 + width) // LIST_ROWS]),
                 in1=wgt_sb[:, c0 : c0 + width],
                 op=MULT,
             )
 
         x_bf = {}
+        x_mx = {}
 
-        def rounded_picks(a, h, tag):
-            x_bf[a, h] = sbuf.tile([P, PACK * HALF], BF16, name="x_bf", tag=tag, align_bytes=MX_ALIGN)
-
-        def round_pair(a, h, u, c0, width, pair=None):
-            if pair is None:
-                pair = picked[a][:, 2 * u : 2 * u + 2, h * HALF + c0 : h * HALF + c0 + width]
+        def round_pair(a, h, u):
             nc.scalar.copy(
-                out=x_bf[a, h][:].rearrange("p (c i) -> p c i", i=PACK)[:, c0 : c0 + width, 2 * u : 2 * u + 2],
-                in_=pair.rearrange("p i c -> p c i"),
-            )
-
-        def round_all(a, h, c0, width):
-            interleave(
-                nc.scalar.copy,
-                x_bf[a, h][:, PACK * c0 : PACK * (c0 + width)],
-                picked[a][:, :, h * HALF + c0 : h * HALF + c0 + width],
+                out=x_bf[a, h].rearrange("p (c i) -> p c i", i=PACK)[:, :, 2 * u : 2 * u + 2],
+                in_=picked[2 * a + u][:, :, h * HALF : (h + 1) * HALF].rearrange("p i c -> p c i"),
             )
 
         def quantise_x(a, h):
-            codes, scales = mx_tiles("x%d%d" % (a, h), HALF)
-            nc.vector.quantize_mx(out=codes[:].bitcast(FP8X4), scales=scales[:], in_=x_bf[a, h][:])
+            codes = shared.tile(
+                [P, HALF], U32, name="x1%d_codes" % h, offset=4 * (PACK * N + HALF * h), align_bytes=MX_ALIGN
+            )
+            scales = tile("x1%d_scales" % h, [HALF], U8)
+            nc.vector.quantize_mx(out=codes[:].bitcast(FP8X4), scales=scales[:], in_=x_bf[a, h])
             x_mx[a, h] = (codes[:].bitcast(FP8X4), scales[:])
 
         def mx_pass(bank, w_slice, a, h, start, stop):
@@ -209,49 +199,19 @@ def tile_list_dl_sigP_kernel(
         def bank(name, h, t):
             return psum.tile([P, HALF], F32, name=name, tag="bank%d" % (PACK * h + t))
 
-        ke = {(h, t): bank("ke", h, t) for h in range(2) for t in range(PACK)}
-
-        for c0 in range(0, J, HALF):
-            pick(0, c0, HALF)
-        for r in range(1, PACK):
-            width = HALF if r == PACK - 1 else J
-            for c0 in range(0, J, width):
-                pick(r, c0, width)
-            if r == 1:
-                for h in range(2):
-                    rounded_picks(0, h, "x_bf0%d" % h)
-                    round_pair(0, h, 0, 0, HALF)
         for h in range(2):
-            round_pair(0, h, 1, 0, HALF)
-            quantise_x(0, h)
-        wk_scales = sbuf.tile([P, N], U8, name="wk_scales", align_bytes=MX_ALIGN)
-        wk_mx = [
-            quantise_weight("wk0", deal_weight("wk0", [(nc.scalar.copy, wk0_in[:])]), wk_scales[:]),
-            quantise_weight(
-                "wk1", deal_weight("wk1", [(nc.scalar.copy, part[:]) for part in wk1_in]), wk_scales[SCALE_ROWS:P, :]
-            ),
-        ]
+            pick(0, h * HALF, HALF)
+        pick(1, 0, J)
+        x_bf0 = tile("x_bf0", [PACK * J], BF16)
         for h in range(2):
-            for t in range(PACK):
-                mx_pass(ke[h, t], wk_mx[0][t], 0, h, True, False)
-        for r in range(PACK, last - 1):
-            pick(r, 0, J)
-        last_pair = sbuf.tile([P, 2, HALF], F32, name="last_pair", tag="x_in0", align_bytes=MX_ALIGN)
-        pick(last - 1, 0, HALF, last_pair[:, 0, :])
-        pick(last - 1, HALF, HALF)
-        rounded_picks(1, 0, "wk1_in1")
-        round_pair(1, 0, 0, 0, HALF)
-        rounded_picks(1, 1, "x_bf11")
-        for c0 in range(0, HALF, QUARTER):
-            pick(last, c0, QUARTER, last_pair[:, 1, c0 : c0 + QUARTER])
-        pick(last, HALF, HALF)
-        for c0 in range(0, HALF, QUARTER):
-            round_pair(1, 0, 1, c0, QUARTER, last_pair[:, :, c0 : c0 + QUARTER])
-        quantise_x(1, 0)
-        round_all(1, 1, 0, HALF)
-        quantise_x(1, 1)
-        v4_words = sbuf.tile([P, PASSES, 2 * N], U8, name="v4_words", tag="x_in0", align_bytes=MX_ALIGN)
-        nc.vector.tensor_copy(
+            x_bf[0, h] = x_bf0[:, h * PACK * HALF : (h + 1) * PACK * HALF]
+            round_pair(0, h, 0)
+        pick(2, 0, J)
+        pick(3, 0, J)
+        for h in range(2):
+            round_pair(0, h, 1)
+        v4_words = tile("v4_words", [PASSES, 2 * N], U8)
+        nc.scalar.copy(
             out=v4_words[:].bitcast(U16).rearrange("p a (t m) -> p a t m", t=PACK),
             in_=v4_words_in[:].bitcast(U16).rearrange("p a (m t) -> p a t m", t=PACK),
         )
@@ -262,40 +222,72 @@ def tile_list_dl_sigP_kernel(
             ]
             for a in range(PASSES)
         ]
-
+        pick(4, 0, J)
+        pick(5, 0, J)
+        codes, scales = quantise("x0", x_bf0[:], "x_in5")
         for h in range(2):
-            for t in range(PACK):
-                mx_pass(ke[h, t], wk_mx[1][t], 1, h, False, True)
+            x_mx[0, h] = (codes[:, h * HALF : (h + 1) * HALF].bitcast(FP8X4), scales[:, h * HALF : (h + 1) * HALF])
 
-        def multiply_by_ke(h, t, out):
-            nc.vector.tensor_tensor(out=out, in0=ke[h, t][:], in1=st_sb[h, t // 2][:, t % 2, :], op=MULT)
+        wk_bf = [tile("wk_bf%d" % a, [PACK * N], BF16) for a in range(PASSES)]
+        deal(nc.scalar.copy, wk_bf[0], wk_in[0], 0, P)
+        for h in range(2):
+            x_bf[1, h] = shared.tile(
+                [P, PACK * HALF], BF16, name="x_bf1%d" % h, offset=2 * PACK * HALF * h, align_bytes=MX_ALIGN
+            )[:]
+            round_pair(1, h, 0)
+        pick(6, 0, J)
+        wk_mx = [slices(*quantise("wk0", wk_bf[0][:], "x_in6"))]
+        for h in range(2):
+            pick(7, h * HALF, HALF)
+            round_pair(1, h, 1)
+        deal(nc.vector.tensor_copy, wk_bf[1], wk_in[1], 0, P)
+        quantise_x(1, 0)
+        wk_mx.append(slices(*quantise("wk1", wk_bf[1][:])))
+        quantise_x(1, 1)
 
-        for h, t in [(h, t) for h in range(2) for t in range(PACK)][:-1]:
-            multiply_by_ke(h, t, st_sb[h, t // 2][:, t % 2, :])
-        wd_scales = [sbuf.tile([P, N], U8, name="wd_scales%d" % a, align_bytes=MX_ALIGN) for a in range(PASSES)]
-        wd_mx = [
-            quantise_weight("wd%d" % a, deal_weight("wd%d" % a, [(nc.scalar.copy, wd_in[a][:])]), wd_scales[a][:])
-            for a in range(PASSES)
-        ]
-        gate = [sbuf.tile([P, PACK + 1 - h, HALF], F32, name="gate", tag="wd_in%d" % (1 - h)) for h in range(2)]
-        last_logit = gate[0][:, PACK, :]
-        multiply_by_ke(1, PACK - 1, last_logit)
-        for h, u in [(0, 0), (0, 1), (1, 0)]:
+        ke = {(h, t): bank("ke", h, t) for h in range(2) for t in range(PACK)}
+        for h in range(2):
+            for a in range(PASSES):
+                for t in range(PACK):
+                    mx_pass(ke[h, t], wk_mx[a][t], a, h, a == 0, a == PASSES - 1)
+
+        gate = [tile("gate%d" % h, [PACK, HALF], F32, tag="x_in%d" % (3 + h)) for h in range(2)]
+
+        def logits(h, u):
+            for v in range(2):
+                nc.vector.tensor_tensor(
+                    out=st_sb[h, u][:, v, :], in0=ke[h, 2 * u + v][:], in1=st_sb[h, u][:, v, :], op=MULT
+                )
+
+        def gates(h, u):
             nc.scalar.activation(out=gate[h][:, 2 * u : 2 * u + 2, :], in_=st_sb[h, u][:], func=SIGMOID)
-        nc.scalar.activation(out=gate[1][:, 2, :], in_=st_sb[1, 1][:, 0, :], func=SIGMOID)
-        nc.scalar.activation(out=gate[1][:, 3, :], in_=last_logit, func=SIGMOID)
 
-        def value_passes(h, t, slot):
-            sums = psum.tile([P, HALF], F32, name="ve", tag="bank%d" % slot)
+        wd_bf = [tile("wd_bf%d" % a, [PACK * N], BF16) for a in range(PASSES)]
+        deal(nc.scalar.copy, wd_bf[0], wd_in[0], 0, P)
+        for u in range(2):
+            logits(0, u)
+        gates(0, 0)
+        wd_mx = [slices(*quantise("wd0", wd_bf[0][:], "st_sb00"))]
+        deal(nc.vector.tensor_copy, wd_bf[1], wd_in[1], 0, VECTOR_SHARE)
+        deal(nc.scalar.copy, wd_bf[1], wd_in[1], VECTOR_SHARE, P)
+        gates(0, 1)
+        wd_mx.append(slices(*quantise("wd1", wd_bf[1][:])))
+        for u in range(2):
+            logits(1, u)
+            gates(1, u)
+
+        def value_passes(h, t):
+            sums = bank("ve", h, t)
             for a in range(PASSES):
                 mx_pass(sums, v4_mx[a][t], a, h, a == 0, False)
             for a in range(PASSES):
                 mx_pass(sums, wd_mx[a][t], a, h, False, a == PASSES - 1)
             return sums
 
-        y_codes, y_scales = mx_tiles("y", J)
+        y_codes = tile("y_codes", [J], U32)
+        y_scales = tile("y_scales", [J], U8)
         words_out = out_1.rearrange("a p j i -> p (a j i)").bitcast(I32)
-        y = [sbuf.tile([P, PACK, HALF], F32, name="y", tag="x_in%d" % (1 + h), align_bytes=MX_ALIGN) for h in range(2)]
+        y = [tile("y%d" % h, [PACK, HALF], F32, tag="x_in%d" % (1 + h)) for h in range(2)]
 
         def result(h, t, c0, width):
             nc.vector.tensor_tensor(
@@ -305,8 +297,8 @@ def tile_list_dl_sigP_kernel(
                 op=MULT,
             )
 
-        def store(h, slices):
-            nc.sync.dma_start(out=out_rows[:, slices, h * HALF : (h + 1) * HALF], in_=y[h][:, slices, :])
+        def store(h, part):
+            nc.sync.dma_start(out=out_rows[:, part, h * HALF : (h + 1) * HALF], in_=y[h][:, part, :])
 
         def gpsimd_copy(out, in_):
             nc.gpsimd.tensor_scalar(
@@ -320,7 +312,7 @@ def tile_list_dl_sigP_kernel(
 
         def rounded(name, h, c0, width, copies):
             share = width // len(copies)
-            y_bf = sbuf.tile([P, PACK * width], BF16, name="y_bf", tag=name, align_bytes=MX_ALIGN)
+            y_bf = tile(name, [PACK * width], BF16)
             for n, copy in enumerate(copies):
                 interleave(
                     copy,
@@ -334,7 +326,7 @@ def tile_list_dl_sigP_kernel(
             nc.vector.quantize_mx(out=y_codes[:, places].bitcast(FP8X4), scales=y_scales[:, places], in_=y_bf[:])
             nc.sync.dma_start(out=words_out[:, places], in_=y_codes[:, places].bitcast(I32))
 
-        ve = {(h, t): value_passes(h, t, PACK * h + t) for h in range(2) for t in range(PACK)}
+        ve = {(h, t): value_passes(h, t) for h in range(2) for t in range(PACK)}
         for h in range(2):
             for t in range(PACK):
                 width = QUARTER if (h, t) == (1, PACK - 1) else HALF

@@ -28,7 +28,7 @@ HEADS = P // LIST_ROWS
 LINE = 4
 HALF = J // 2
 QUARTER = J // 4
-VECTOR_SHARE = 96
+SCALAR_SHARE = 80
 MX_ALIGN = 64
 
 
@@ -37,6 +37,10 @@ def interleave(copy, out, rows):
         out=out.rearrange("p (b c i) -> p b i c", c=LINE, i=PACK),
         in_=rows.rearrange("p i (b c) -> p b i c", c=LINE),
     )
+
+
+def st_at(h, t):
+    return 4 * HALF * (PACK * h + t)
 
 
 def scale_rows(quad):
@@ -65,7 +69,7 @@ def tile_list_dl_sigP_kernel(
 
         runs = HALF // P
         wgt_rows = tile("wgt_rows", [P], F32)
-        nc.sync.dma_start(
+        nc.scalar.dma_start(
             out=wgt_rows[0 : runs * HEADS, :],
             in_=wgt[:, HALF:J].rearrange("(g r) (s c) -> r g s c", r=LIST_ROWS, c=P)[0],
         )
@@ -79,7 +83,8 @@ def tile_list_dl_sigP_kernel(
         v4_scales = tile("v4_scales", [PASSES, N], U8)
         nc.vector.memset(v4_scales_in[:].bitcast(I32), 0)
         for quad in range(QUADRANTS):
-            nc.scalar.dma_start(
+            queue = nc.sync if quad < QUADRANTS // 2 else nc.scalar
+            queue.dma_start(
                 out=v4_rows[scale_partitions(quad), :, :].bitcast(I32),
                 in_=wv4_scales[:, scale_rows(quad), :].bitcast(I32).rearrange("a r w -> r a w"),
             )
@@ -97,15 +102,23 @@ def tile_list_dl_sigP_kernel(
         nc.scalar.activation(out=warm[:, 1:2], in_=warm[:, 0:1], func=SIGMOID)
 
         windows = PASSES * PACK
-        wgt_sb = tile("wgt_sb", [J], F32)
+        picked = [tile("picked%d" % pair, [2, J], F32) for pair in range(2)]
+        late = tile("late", [PACK * J], F32)
+        late_rows = late[:].rearrange("p (i c) -> p i c", i=PACK)
+        wgt_sb = late[:, 2 * J + HALF : 3 * J + HALF]
+        last_pair = tile("last_pair", [2, HALF], F32)
         v4_words_in = tile("v4_words_in", [PASSES, 2 * N], U8)
         x_in = [tile("x_in%d" % r, [T], F32) for r in range(windows)]
-        wk_in = [
-            shared.tile([P, PACK, N], F32, name="wk_in0", offset=0, align_bytes=MX_ALIGN),
-            shared.tile([P, PACK, N], F32, name="wk_in1", offset=4 * PACK * N, align_bytes=MX_ALIGN),
-        ]
+        wk0_in = [tile("wk0_in%d" % u, [2, N], F32) for u in range(2)]
+        wk1_in = tile("wk1_in", [PACK, N], F32)
         wd_in = [tile("wd_in%d" % a, [PACK, N], F32) for a in range(PASSES)]
-        st_sb = {(h, u): tile("st_sb%d%d" % (h, u), [2, HALF], F32) for h in range(2) for u in range(2)}
+        st_parts = [(0, 0, 2), (0, 2, 4), (1, 0, 2), (1, 2, 3), (1, 3, 4)]
+        st_sb = {
+            (h, t0): shared.tile(
+                [P, t1 - t0, HALF], F32, name="st_sb%d%d" % (h, t0), offset=st_at(h, t0), align_bytes=MX_ALIGN
+            )
+            for h, t0, t1 in st_parts
+        }
         x_rows = xT.rearrange("(a p i) c -> a i p c", p=P, i=PACK)
         wk_rows = wk.rearrange("(a p i) n -> a p i n", p=P, i=PACK)
         wd_rows = wvd.rearrange("(a p i) n -> a p i n", p=P, i=PACK)
@@ -117,16 +130,19 @@ def tile_list_dl_sigP_kernel(
                 nc.sync.dma_start(out=x_in[r][:], in_=x_rows[r // PACK, r % PACK])
 
         def load_st(h):
-            for u in range(2):
-                nc.sync.dma_start(out=st_sb[h, u][:], in_=st_rows[:, 2 * u : 2 * u + 2, h * HALF : (h + 1) * HALF])
+            for t0, t1 in [part[1:] for part in st_parts if part[0] == h]:
+                nc.sync.dma_start(out=st_sb[h, t0][:], in_=st_rows[:, t0:t1, h * HALF : (h + 1) * HALF])
 
-        nc.sync.dma_start(out=wgt_sb[:, 0:HALF], in_=wgt[:, 0:HALF])
-        load_x(0, PACK + 1)
+        nc.sync.dma_start(out=wgt_sb[:, 0:P], in_=wgt[:, 0:P])
+        load_x(0, 1)
+        nc.sync.dma_start(out=wgt_sb[:, P:HALF], in_=wgt[:, P:HALF])
+        load_x(1, windows - 2)
+        nc.sync.dma_start(out=wk0_in[0][:], in_=wk_rows[0][:, 0:2])
+        load_x(windows - 2, windows - 1)
+        nc.sync.dma_start(out=wk0_in[1][:], in_=wk_rows[0][:, 2:PACK])
+        load_x(windows - 1, windows)
+        nc.sync.dma_start(out=wk1_in[:], in_=wk_rows[1])
         nc.sync.dma_start(out=v4_words_in[:].bitcast(I32), in_=wv4_words.bitcast(I32).rearrange("a p w -> p a w"))
-        load_x(PACK + 1, windows - 2)
-        nc.sync.dma_start(out=wk_in[0][:], in_=wk_rows[0])
-        load_x(windows - 2, windows)
-        nc.sync.dma_start(out=wk_in[1][:], in_=wk_rows[1])
         nc.sync.dma_start(out=wd_in[0][:], in_=wd_rows[0])
         load_st(0)
         nc.sync.dma_start(out=wd_in[1][:], in_=wd_rows[1])
@@ -148,9 +164,12 @@ def tile_list_dl_sigP_kernel(
                 in_=w_in[:].rearrange("p i (m t) -> p m i t", t=PACK)[:, m0:m1],
             )
 
-        def quantise(name, values, tag=None):
+        def quantise(name, values, tag=None, offset=None):
             width = values.shape[1] // PACK
-            codes = tile(name + "_codes", [width], U32, tag)
+            if offset is None:
+                codes = tile(name + "_codes", [width], U32, tag)
+            else:
+                codes = shared.tile([P, width], U32, name=name + "_codes", offset=offset, align_bytes=MX_ALIGN)
             scales = tile(name + "_scales", [width], U8)[:]
             nc.vector.quantize_mx(out=codes[:].bitcast(FP8X4), scales=scales, in_=values)
             return codes, scales
@@ -158,32 +177,40 @@ def tile_list_dl_sigP_kernel(
         def slices(codes, scales):
             return [(codes[:, P * t : P * (t + 1)].bitcast(FP8X4), scales[:, P * t : P * (t + 1)]) for t in range(PACK)]
 
-        picked = [tile("picked%d" % pair, [2, J], F32) for pair in range(windows // 2)]
 
-        def pick(r, c0, width):
+        def pick(r, c0, width, out=None):
+            if out is None:
+                rows = picked[r // 2][:, r % 2] if r < PACK else late_rows[:, r - PACK]
+                out = rows[:, c0 : c0 + width]
             nc.vector.tensor_tensor(
-                out=picked[r // 2][:, r % 2, c0 : c0 + width],
+                out=out,
                 in0=x_in[r][:].indirect(offsets[:, c0 // LIST_ROWS : (c0 + width) // LIST_ROWS]),
                 in1=wgt_sb[:, c0 : c0 + width],
                 op=MULT,
             )
 
+        def gpsimd_copy(out, in_):
+            nc.gpsimd.tensor_scalar(
+                out=out.rearrange("p b i c -> p b c i"),
+                in0=in_.rearrange("p b i c -> p b c i"),
+                scalar1=1.0,
+                scalar2=-0.0,
+                op0=MULT,
+                op1=ADD,
+            )
+
         x_bf = {}
         x_mx = {}
 
-        def round_pair(a, h, u):
+        def round_pair(a, h, u, pair):
             nc.scalar.copy(
                 out=x_bf[a, h].rearrange("p (c i) -> p c i", i=PACK)[:, :, 2 * u : 2 * u + 2],
-                in_=picked[2 * a + u][:, :, h * HALF : (h + 1) * HALF].rearrange("p i c -> p c i"),
+                in_=pair.rearrange("p i c -> p c i"),
             )
 
-        def quantise_x(a, h):
-            codes = shared.tile(
-                [P, HALF], U32, name="x1%d_codes" % h, offset=4 * (PACK * N + HALF * h), align_bytes=MX_ALIGN
-            )
-            scales = tile("x1%d_scales" % h, [HALF], U8)
-            nc.vector.quantize_mx(out=codes[:].bitcast(FP8X4), scales=scales[:], in_=x_bf[a, h])
-            x_mx[a, h] = (codes[:].bitcast(FP8X4), scales[:])
+        def quantise_x(a, h, offset=None):
+            codes, scales = quantise("x%d%d" % (a, h), x_bf[a, h], offset=offset)
+            x_mx[a, h] = (codes[:].bitcast(FP8X4), scales)
 
         def mx_pass(bank, w_slice, a, h, start, stop):
             nc.tensor.matmul_mx(
@@ -199,17 +226,66 @@ def tile_list_dl_sigP_kernel(
         def bank(name, h, t):
             return psum.tile([P, HALF], F32, name=name, tag="bank%d" % (PACK * h + t))
 
-        for h in range(2):
-            pick(0, h * HALF, HALF)
+        for c0, c1 in ((0, P), (P, HALF), (HALF, J)):
+            pick(0, c0, c1 - c0)
         pick(1, 0, J)
         x_bf0 = tile("x_bf0", [PACK * J], BF16)
         for h in range(2):
             x_bf[0, h] = x_bf0[:, h * PACK * HALF : (h + 1) * PACK * HALF]
-            round_pair(0, h, 0)
+            round_pair(0, h, 0, picked[0][:, :, h * HALF : (h + 1) * HALF])
         pick(2, 0, J)
         pick(3, 0, J)
         for h in range(2):
-            round_pair(0, h, 1)
+            round_pair(0, h, 1, picked[1][:, :, h * HALF : (h + 1) * HALF])
+        pick(4, 0, J)
+        pick(5, 0, J)
+        codes, scales = quantise("x0", x_bf0[:], "x_in5")
+        for h in range(2):
+            x_mx[0, h] = (codes[:, h * HALF : (h + 1) * HALF].bitcast(FP8X4), scales[:, h * HALF : (h + 1) * HALF])
+
+        wk_bf = [tile("wk_bf%d" % a, [PACK * N], BF16) for a in range(PASSES)]
+        for u in range(2):
+            nc.scalar.copy(
+                out=wk_bf[0][:].rearrange("p (t m i) -> p m i t", t=PACK, i=PACK)[:, :, 2 * u : 2 * u + 2],
+                in_=wk0_in[u][:].rearrange("p i (m t) -> p m i t", t=PACK),
+            )
+        x_bf[1, 0] = tile("x_bf10", [PACK * HALF], BF16, "wk0_in1")[:]
+        round_pair(1, 0, 0, late_rows[:, 0:2, 0:HALF])
+        pick(6, 0, HALF, last_pair[:, 0, :])
+        wk_mx = [slices(*quantise("wk0", wk_bf[0][:]))]
+        pick(7, 0, HALF, last_pair[:, 1, :])
+        round_pair(1, 0, 1, last_pair[:])
+        pick(7, HALF, HALF)
+        pick(6, HALF, HALF)
+        quantise_x(1, 0)
+        deal(nc.scalar.copy, wk_bf[1], wk1_in, 0, SCALAR_SHARE)
+        deal(nc.vector.tensor_copy, wk_bf[1], wk1_in, SCALAR_SHARE, P)
+        wk_mx.append(slices(*quantise("wk1", wk_bf[1][:])))
+        x_bf[1, 1] = tile("x_bf11", [PACK * HALF], BF16, "wk_bf1")[:]
+        interleave(gpsimd_copy, x_bf[1, 1], late_rows[:, :, HALF:J])
+
+        ke = {(h, t): bank("ke", h, t) for h in range(2) for t in range(PACK)}
+
+        def key_passes(a, h):
+            for t in range(PACK):
+                mx_pass(ke[h, t], wk_mx[a][t], a, h, a == 0, a == PASSES - 1)
+
+        key_passes(0, 0)
+        key_passes(1, 0)
+        key_passes(0, 1)
+
+        logit = [tile("logit%d" % h, [PACK, HALF], F32, tag="x_in%d" % (3 + h)) for h in range(2)]
+        gate = {}
+
+        def logits(h, t0, t1):
+            for t in range(t0, t1):
+                nc.vector.tensor_tensor(out=logit[h][:, t, :], in0=ke[h, t][:], in1=st_sb[h, t0][:, t - t0, :], op=MULT)
+
+        def gates(h, u, out=None):
+            pair = logit[h][:, 2 * u : 2 * u + 2, :]
+            gate[h, u] = pair if out is None else out
+            nc.scalar.activation(out=gate[h, u], in_=pair, func=SIGMOID)
+
         v4_words = tile("v4_words", [PASSES, 2 * N], U8)
         nc.scalar.copy(
             out=v4_words[:].bitcast(U16).rearrange("p a (t m) -> p a t m", t=PACK),
@@ -222,66 +298,30 @@ def tile_list_dl_sigP_kernel(
             ]
             for a in range(PASSES)
         ]
-        pick(4, 0, J)
-        pick(5, 0, J)
-        codes, scales = quantise("x0", x_bf0[:], "x_in5")
-        for h in range(2):
-            x_mx[0, h] = (codes[:, h * HALF : (h + 1) * HALF].bitcast(FP8X4), scales[:, h * HALF : (h + 1) * HALF])
-
-        wk_bf = [tile("wk_bf%d" % a, [PACK * N], BF16) for a in range(PASSES)]
-        deal(nc.scalar.copy, wk_bf[0], wk_in[0], 0, P)
-        for h in range(2):
-            x_bf[1, h] = shared.tile(
-                [P, PACK * HALF], BF16, name="x_bf1%d" % h, offset=2 * PACK * HALF * h, align_bytes=MX_ALIGN
-            )[:]
-            round_pair(1, h, 0)
-        pick(6, 0, J)
-        wk_mx = [slices(*quantise("wk0", wk_bf[0][:], "x_in6"))]
-        for h in range(2):
-            pick(7, h * HALF, HALF)
-            round_pair(1, h, 1)
-        deal(nc.vector.tensor_copy, wk_bf[1], wk_in[1], 0, P)
-        quantise_x(1, 0)
-        wk_mx.append(slices(*quantise("wk1", wk_bf[1][:])))
-        quantise_x(1, 1)
-
-        ke = {(h, t): bank("ke", h, t) for h in range(2) for t in range(PACK)}
-        for h in range(2):
-            for a in range(PASSES):
-                for t in range(PACK):
-                    mx_pass(ke[h, t], wk_mx[a][t], a, h, a == 0, a == PASSES - 1)
-
-        gate = [tile("gate%d" % h, [PACK, HALF], F32, tag="x_in%d" % (3 + h)) for h in range(2)]
-
-        def logits(h, u):
-            for v in range(2):
-                nc.vector.tensor_tensor(
-                    out=st_sb[h, u][:, v, :], in0=ke[h, 2 * u + v][:], in1=st_sb[h, u][:, v, :], op=MULT
-                )
-
-        def gates(h, u):
-            nc.scalar.activation(out=gate[h][:, 2 * u : 2 * u + 2, :], in_=st_sb[h, u][:], func=SIGMOID)
-
         wd_bf = [tile("wd_bf%d" % a, [PACK * N], BF16) for a in range(PASSES)]
         deal(nc.scalar.copy, wd_bf[0], wd_in[0], 0, P)
-        for u in range(2):
-            logits(0, u)
+        logits(0, 0, 2)
         gates(0, 0)
-        wd_mx = [slices(*quantise("wd0", wd_bf[0][:], "st_sb00"))]
-        deal(nc.vector.tensor_copy, wd_bf[1], wd_in[1], 0, VECTOR_SHARE)
-        deal(nc.scalar.copy, wd_bf[1], wd_in[1], VECTOR_SHARE, P)
-        gates(0, 1)
-        wd_mx.append(slices(*quantise("wd1", wd_bf[1][:])))
-        for u in range(2):
-            logits(1, u)
-            gates(1, u)
+        logits(0, 2, 4)
+        quantise_x(1, 1, st_at(0, 2))
+        key_passes(1, 1)
+        wd_mx = [slices(*quantise("wd0", wd_bf[0][:], offset=st_at(0, 3)))]
+        deal(nc.scalar.copy, wd_bf[1], wd_in[1], 0, P)
+        gates(0, 1, tile("gate01", [2, HALF], F32, "wd_in1")[:])
+        logits(1, 0, 2)
+        gates(1, 0)
+        logits(1, 2, 3)
+        wd_mx.append(slices(*quantise("wd1", wd_bf[1][:], offset=st_at(1, 2))))
+        logits(1, 3, 4)
+        gates(1, 1)
 
         def value_passes(h, t):
             sums = bank("ve", h, t)
-            for a in range(PASSES):
-                mx_pass(sums, v4_mx[a][t], a, h, a == 0, False)
-            for a in range(PASSES):
-                mx_pass(sums, wd_mx[a][t], a, h, False, a == PASSES - 1)
+            terms = [(w[a][t], a) for w in (v4_mx, wd_mx) for a in range(PASSES)]
+            if (h, t // 2) == (1, 1):
+                terms = terms[::-1]
+            for n, (w_slice, a) in enumerate(terms):
+                mx_pass(sums, w_slice, a, h, n == 0, n == len(terms) - 1)
             return sums
 
         y_codes = tile("y_codes", [J], U32)
@@ -293,22 +333,12 @@ def tile_list_dl_sigP_kernel(
             nc.vector.tensor_tensor(
                 out=y[h][:, t, c0 : c0 + width],
                 in0=ve[h, t][:, c0 : c0 + width],
-                in1=gate[h][:, t, c0 : c0 + width],
+                in1=gate[h, t // 2][:, t % 2, c0 : c0 + width],
                 op=MULT,
             )
 
         def store(h, part):
             nc.sync.dma_start(out=out_rows[:, part, h * HALF : (h + 1) * HALF], in_=y[h][:, part, :])
-
-        def gpsimd_copy(out, in_):
-            nc.gpsimd.tensor_scalar(
-                out=out.rearrange("p b i c -> p b c i"),
-                in0=in_.rearrange("p b i c -> p b c i"),
-                scalar1=1.0,
-                scalar2=-0.0,
-                op0=MULT,
-                op1=ADD,
-            )
 
         def rounded(name, h, c0, width, copies):
             share = width // len(copies)

@@ -28,7 +28,6 @@ HEADS = P // LIST_ROWS
 LINE = 4
 HALF = J // 2
 QUARTER = J // 4
-SCALAR_SHARE = 80
 MX_ALIGN = 64
 
 
@@ -37,10 +36,6 @@ def interleave(copy, out, rows):
         out=out.rearrange("p (b c i) -> p b i c", c=LINE, i=PACK),
         in_=rows.rearrange("p i (b c) -> p b i c", c=LINE),
     )
-
-
-def st_at(h, t):
-    return 4 * HALF * (PACK * h + t)
 
 
 def scale_rows(quad):
@@ -58,7 +53,6 @@ def tile_list_dl_sigP_kernel(
     nc = tc.nc
     with ExitStack() as ctx:
         sbuf = ctx.enter_context(tc.tile_pool(name="sbuf", bufs=1))
-        shared = ctx.enter_context(tc.tile_pool(name="shared", bufs=1))
         psum = ctx.enter_context(tc.psum_pool(name="psum", bufs=1))
 
         def tile(name, shape, dtype, tag=None):
@@ -67,14 +61,13 @@ def tile_list_dl_sigP_kernel(
         offsets = sbuf.tile([P, J // LIST_ROWS], U16, name="offsets")
         nc.sync.dma_start(offsets[:], offs)
 
-        runs = HALF // P
+        runs = J // P
         wgt_rows = tile("wgt_rows", [P], F32)
-        nc.scalar.dma_start(
+        nc.sync.dma_start(
             out=wgt_rows[0 : runs * HEADS, :],
-            in_=wgt[:, HALF:J].rearrange("(g r) (s c) -> r g s c", r=LIST_ROWS, c=P)[0],
+            in_=wgt.rearrange("(g r) (s c) -> r g s c", r=LIST_ROWS, c=P)[0],
         )
-        nc.vector.memset(wgt_rows[P // 4 : P // 2, :], 0.0)
-        nc.vector.memset(wgt_rows[P // 2 : P, :], 0.0)
+        nc.vector.memset(wgt_rows[runs * HEADS : P, :], 0.0)
         identity = tile("identity", [P], F32)
         make_identity(nc, identity[:])
 
@@ -102,23 +95,14 @@ def tile_list_dl_sigP_kernel(
         nc.scalar.activation(out=warm[:, 1:2], in_=warm[:, 0:1], func=SIGMOID)
 
         windows = PASSES * PACK
-        picked = [tile("picked%d" % pair, [2, J], F32) for pair in range(2)]
-        late = tile("late", [PACK * J], F32)
-        late_rows = late[:].rearrange("p (i c) -> p i c", i=PACK)
-        wgt_sb = late[:, 2 * J + HALF : 3 * J + HALF]
+        picked = [tile("picked%d" % a, [PACK, J], F32) for a in range(PASSES)]
         last_pair = tile("last_pair", [2, HALF], F32)
+        wgt_sb = tile("wgt_sb", [J], F32)
         v4_words_in = tile("v4_words_in", [PASSES, 2 * N], U8)
         x_in = [tile("x_in%d" % r, [T], F32) for r in range(windows)]
-        wk0_in = [tile("wk0_in%d" % u, [2, N], F32) for u in range(2)]
-        wk1_in = tile("wk1_in", [PACK, N], F32)
+        wk_in = [tile("wk_in%d" % a, [PACK, N], F32) for a in range(PASSES)]
         wd_in = [tile("wd_in%d" % a, [PACK, N], F32) for a in range(PASSES)]
-        st_parts = [(0, 0, 2), (0, 2, 4), (1, 0, 2), (1, 2, 3), (1, 3, 4)]
-        st_sb = {
-            (h, t0): shared.tile(
-                [P, t1 - t0, HALF], F32, name="st_sb%d%d" % (h, t0), offset=st_at(h, t0), align_bytes=MX_ALIGN
-            )
-            for h, t0, t1 in st_parts
-        }
+        st_sb = {(h, u): tile("st_sb%d%d" % (h, u), [2, HALF], F32) for h in range(2) for u in range(2)}
         x_rows = xT.rearrange("(a p i) c -> a i p c", p=P, i=PACK)
         wk_rows = wk.rearrange("(a p i) n -> a p i n", p=P, i=PACK)
         wd_rows = wvd.rearrange("(a p i) n -> a p i n", p=P, i=PACK)
@@ -130,46 +114,43 @@ def tile_list_dl_sigP_kernel(
                 nc.sync.dma_start(out=x_in[r][:], in_=x_rows[r // PACK, r % PACK])
 
         def load_st(h):
-            for t0, t1 in [part[1:] for part in st_parts if part[0] == h]:
-                nc.sync.dma_start(out=st_sb[h, t0][:], in_=st_rows[:, t0:t1, h * HALF : (h + 1) * HALF])
+            for u in range(2):
+                nc.sync.dma_start(out=st_sb[h, u][:], in_=st_rows[:, 2 * u : 2 * u + 2, h * HALF : (h + 1) * HALF])
 
-        nc.sync.dma_start(out=wgt_sb[:, 0:P], in_=wgt[:, 0:P])
-        load_x(0, 1)
-        nc.sync.dma_start(out=wgt_sb[:, P:HALF], in_=wgt[:, P:HALF])
-        load_x(1, windows - 2)
-        nc.sync.dma_start(out=wk0_in[0][:], in_=wk_rows[0][:, 0:2])
-        load_x(windows - 2, windows - 1)
-        nc.sync.dma_start(out=wk0_in[1][:], in_=wk_rows[0][:, 2:PACK])
-        load_x(windows - 1, windows)
-        nc.sync.dma_start(out=wk1_in[:], in_=wk_rows[1])
+        load_x(0, windows - 2)
+        for a in range(PASSES):
+            nc.sync.dma_start(out=wk_in[a][:], in_=wk_rows[a])
+            load_x(windows - 2 + a, windows - 1 + a)
         nc.sync.dma_start(out=v4_words_in[:].bitcast(I32), in_=wv4_words.bitcast(I32).rearrange("a p w -> p a w"))
-        nc.sync.dma_start(out=wd_in[0][:], in_=wd_rows[0])
         load_st(0)
+        nc.sync.dma_start(out=wd_in[0][:], in_=wd_rows[0])
         nc.sync.dma_start(out=wd_in[1][:], in_=wd_rows[1])
         load_st(1)
 
         turned = psum.tile([P, P], F32, name="turned", tag="bank0")
         nc.tensor.transpose(turned[:], wgt_rows[:], identity[:])
-        repeated = tile("repeated", [runs, HEADS, LIST_ROWS], F32)
         by_head = turned[:, 0 : runs * HEADS].rearrange("p (g s) -> p s g", g=HEADS).unsqueeze(3)
-        nc.scalar.copy(out=repeated[:], in_=by_head.to_broadcast([P, runs, HEADS, LIST_ROWS]))
-        back = psum.tile([P, runs, P], F32, name="back", tag="bank1")
-        for s in range(runs):
-            nc.tensor.transpose(back[:, s, :], repeated[:, s].rearrange("p g r -> p (g r)"), identity[:])
-        nc.scalar.copy(out=wgt_sb[:, HALF:J], in_=back[:].rearrange("p s c -> p (s c)"))
+        half_runs = runs // 2
+        for h in range(2):
+            repeated = tile("repeated%d" % h, [half_runs, HEADS, LIST_ROWS], F32)
+            nc.scalar.copy(
+                out=repeated[:],
+                in_=by_head[:, h * half_runs : (h + 1) * half_runs].to_broadcast([P, half_runs, HEADS, LIST_ROWS]),
+            )
+            back = psum.tile([P, half_runs, P], F32, name="back", tag="bank%d" % (1 + h))
+            for s in range(half_runs):
+                nc.tensor.transpose(back[:, s, :], repeated[:, s].rearrange("p g r -> p (g r)"), identity[:])
+            nc.scalar.copy(out=wgt_sb[:, h * HALF : (h + 1) * HALF], in_=back[:].rearrange("p s c -> p (s c)"))
 
-        def deal(copy, w_bf, w_in, m0, m1):
+        def deal(copy, w_bf, columns, m0=0):
             copy(
-                out=w_bf[:].rearrange("p (t m i) -> p m i t", t=PACK, i=PACK)[:, m0:m1],
-                in_=w_in[:].rearrange("p i (m t) -> p m i t", t=PACK)[:, m0:m1],
+                out=w_bf[:].rearrange("p (t m i) -> p m i t", t=PACK, i=PACK)[:, m0 : m0 + columns.shape[2] // PACK],
+                in_=columns.rearrange("p i (m t) -> p m i t", t=PACK),
             )
 
-        def quantise(name, values, tag=None, offset=None):
+        def quantise(name, values, tag=None):
             width = values.shape[1] // PACK
-            if offset is None:
-                codes = tile(name + "_codes", [width], U32, tag)
-            else:
-                codes = shared.tile([P, width], U32, name=name + "_codes", offset=offset, align_bytes=MX_ALIGN)
+            codes = tile(name + "_codes", [width], U32, tag)
             scales = tile(name + "_scales", [width], U8)[:]
             nc.vector.quantize_mx(out=codes[:].bitcast(FP8X4), scales=scales, in_=values)
             return codes, scales
@@ -179,11 +160,8 @@ def tile_list_dl_sigP_kernel(
 
 
         def pick(r, c0, width, out=None):
-            if out is None:
-                rows = picked[r // 2][:, r % 2] if r < PACK else late_rows[:, r - PACK]
-                out = rows[:, c0 : c0 + width]
             nc.vector.tensor_tensor(
-                out=out,
+                out=picked[r // PACK][:, r % PACK, c0 : c0 + width] if out is None else out,
                 in0=x_in[r][:].indirect(offsets[:, c0 // LIST_ROWS : (c0 + width) // LIST_ROWS]),
                 in1=wgt_sb[:, c0 : c0 + width],
                 op=MULT,
@@ -202,14 +180,16 @@ def tile_list_dl_sigP_kernel(
         x_bf = {}
         x_mx = {}
 
-        def round_pair(a, h, u, pair):
+        def round_pair(a, h, u, c0=0, width=HALF, pair=None):
+            if pair is None:
+                pair = picked[a][:, 2 * u : 2 * u + 2, h * HALF + c0 : h * HALF + c0 + width]
             nc.scalar.copy(
-                out=x_bf[a, h].rearrange("p (c i) -> p c i", i=PACK)[:, :, 2 * u : 2 * u + 2],
+                out=x_bf[a, h].rearrange("p (c i) -> p c i", i=PACK)[:, c0 : c0 + width, 2 * u : 2 * u + 2],
                 in_=pair.rearrange("p i c -> p c i"),
             )
 
-        def quantise_x(a, h, offset=None):
-            codes, scales = quantise("x%d%d" % (a, h), x_bf[a, h], offset=offset)
+        def quantise_x(a, h, tag=None):
+            codes, scales = quantise("x%d%d" % (a, h), x_bf[a, h], tag)
             x_mx[a, h] = (codes[:].bitcast(FP8X4), scales)
 
         def mx_pass(bank, w_slice, a, h, start, stop):
@@ -226,17 +206,17 @@ def tile_list_dl_sigP_kernel(
         def bank(name, h, t):
             return psum.tile([P, HALF], F32, name=name, tag="bank%d" % (PACK * h + t))
 
-        for c0, c1 in ((0, P), (P, HALF), (HALF, J)):
-            pick(0, c0, c1 - c0)
+        for h in range(2):
+            pick(0, h * HALF, HALF)
         pick(1, 0, J)
         x_bf0 = tile("x_bf0", [PACK * J], BF16)
         for h in range(2):
             x_bf[0, h] = x_bf0[:, h * PACK * HALF : (h + 1) * PACK * HALF]
-            round_pair(0, h, 0, picked[0][:, :, h * HALF : (h + 1) * HALF])
+            round_pair(0, h, 0)
         pick(2, 0, J)
         pick(3, 0, J)
         for h in range(2):
-            round_pair(0, h, 1, picked[1][:, :, h * HALF : (h + 1) * HALF])
+            round_pair(0, h, 1)
         pick(4, 0, J)
         pick(5, 0, J)
         codes, scales = quantise("x0", x_bf0[:], "x_in5")
@@ -244,50 +224,23 @@ def tile_list_dl_sigP_kernel(
             x_mx[0, h] = (codes[:, h * HALF : (h + 1) * HALF].bitcast(FP8X4), scales[:, h * HALF : (h + 1) * HALF])
 
         wk_bf = [tile("wk_bf%d" % a, [PACK * N], BF16) for a in range(PASSES)]
-        for u in range(2):
-            nc.scalar.copy(
-                out=wk_bf[0][:].rearrange("p (t m i) -> p m i t", t=PACK, i=PACK)[:, :, 2 * u : 2 * u + 2],
-                in_=wk0_in[u][:].rearrange("p i (m t) -> p m i t", t=PACK),
-            )
-        x_bf[1, 0] = tile("x_bf10", [PACK * HALF], BF16, "wk0_in1")[:]
-        round_pair(1, 0, 0, late_rows[:, 0:2, 0:HALF])
+        deal(nc.scalar.copy, wk_bf[0], wk_in[0][:])
+        x_bf[1, 0] = tile("x_bf10", [PACK * HALF], BF16, "wk_in0")[:]
+        round_pair(1, 0, 0)
+        deal(nc.scalar.copy, wk_bf[1], wk_in[1][:])
         pick(6, 0, HALF, last_pair[:, 0, :])
-        wk_mx = [slices(*quantise("wk0", wk_bf[0][:]))]
-        pick(7, 0, HALF, last_pair[:, 1, :])
-        round_pair(1, 0, 1, last_pair[:])
-        pick(7, HALF, HALF)
         pick(6, HALF, HALF)
+        wk_mx = [slices(*quantise("wk0", wk_bf[0][:], "x_in6"))]
+        for c0 in range(0, HALF, QUARTER):
+            pick(7, c0, QUARTER, last_pair[:, 1, c0 : c0 + QUARTER])
+            round_pair(1, 0, 1, c0, QUARTER, last_pair[:, :, c0 : c0 + QUARTER])
+        pick(7, HALF, HALF)
+        wk_mx.append(slices(*quantise("wk1", wk_bf[1][:], "x_in7")))
         quantise_x(1, 0)
-        deal(nc.scalar.copy, wk_bf[1], wk1_in, 0, SCALAR_SHARE)
-        deal(nc.vector.tensor_copy, wk_bf[1], wk1_in, SCALAR_SHARE, P)
-        wk_mx.append(slices(*quantise("wk1", wk_bf[1][:])))
-        x_bf[1, 1] = tile("x_bf11", [PACK * HALF], BF16, "wk_bf1")[:]
-        interleave(gpsimd_copy, x_bf[1, 1], late_rows[:, :, HALF:J])
-
-        ke = {(h, t): bank("ke", h, t) for h in range(2) for t in range(PACK)}
-
-        def key_passes(a, h):
-            for t in range(PACK):
-                mx_pass(ke[h, t], wk_mx[a][t], a, h, a == 0, a == PASSES - 1)
-
-        key_passes(0, 0)
-        key_passes(1, 0)
-        key_passes(0, 1)
-
-        logit = [tile("logit%d" % h, [PACK, HALF], F32, tag="x_in%d" % (3 + h)) for h in range(2)]
-        gate = {}
-
-        def logits(h, t0, t1):
-            for t in range(t0, t1):
-                nc.vector.tensor_tensor(out=logit[h][:, t, :], in0=ke[h, t][:], in1=st_sb[h, t0][:, t - t0, :], op=MULT)
-
-        def gates(h, u, out=None):
-            pair = logit[h][:, 2 * u : 2 * u + 2, :]
-            gate[h, u] = pair if out is None else out
-            nc.scalar.activation(out=gate[h, u], in_=pair, func=SIGMOID)
-
-        v4_words = tile("v4_words", [PASSES, 2 * N], U8)
-        nc.scalar.copy(
+        x_bf[1, 1] = tile("x_bf11", [PACK * HALF], BF16)[:]
+        interleave(nc.scalar.copy, x_bf[1, 1], picked[1][:, :, HALF:J])
+        v4_words = tile("v4_words", [PASSES, 2 * N], U8, "last_pair")
+        nc.vector.tensor_copy(
             out=v4_words[:].bitcast(U16).rearrange("p a (t m) -> p a t m", t=PACK),
             in_=v4_words_in[:].bitcast(U16).rearrange("p a (m t) -> p a t m", t=PACK),
         )
@@ -298,22 +251,38 @@ def tile_list_dl_sigP_kernel(
             ]
             for a in range(PASSES)
         ]
+        quantise_x(1, 1)
+
+        ke = {(h, t): bank("ke", h, t) for h in range(2) for t in range(PACK)}
+        for h in range(2):
+            for a in range(PASSES):
+                for t in range(PACK):
+                    mx_pass(ke[h, t], wk_mx[a][t], a, h, a == 0, a == PASSES - 1)
+
+        gate = [tile("gate%d" % h, [PACK, HALF], F32, tag="wd_in%d" % (1 - h)) for h in range(2)]
+
+        def logits(h, u):
+            for v in range(2):
+                nc.vector.tensor_tensor(
+                    out=st_sb[h, u][:, v, :], in0=ke[h, 2 * u + v][:], in1=st_sb[h, u][:, v, :], op=MULT
+                )
+
+        def gates(h, u):
+            nc.scalar.activation(out=gate[h][:, 2 * u : 2 * u + 2, :], in_=st_sb[h, u][:], func=SIGMOID)
+
         wd_bf = [tile("wd_bf%d" % a, [PACK * N], BF16) for a in range(PASSES)]
-        deal(nc.scalar.copy, wd_bf[0], wd_in[0], 0, P)
-        logits(0, 0, 2)
-        gates(0, 0)
-        logits(0, 2, 4)
-        quantise_x(1, 1, st_at(0, 2))
-        key_passes(1, 1)
-        wd_mx = [slices(*quantise("wd0", wd_bf[0][:], offset=st_at(0, 3)))]
-        deal(nc.scalar.copy, wd_bf[1], wd_in[1], 0, P)
-        gates(0, 1, tile("gate01", [2, HALF], F32, "wd_in1")[:])
-        logits(1, 0, 2)
-        gates(1, 0)
-        logits(1, 2, 3)
-        wd_mx.append(slices(*quantise("wd1", wd_bf[1][:], offset=st_at(1, 2))))
-        logits(1, 3, 4)
-        gates(1, 1)
+        for u in range(2):
+            logits(0, u)
+        wd_mx = []
+        for a in range(PASSES):
+            deal(nc.scalar.copy, wd_bf[a], wd_in[a][:])
+            if a == PASSES - 1:
+                logits(1, 0)
+            wd_mx.append(slices(*quantise("wd%d" % a, wd_bf[a][:])))
+        logits(1, 1)
+        for h in range(2):
+            for u in range(2):
+                gates(h, u)
 
         def value_passes(h, t):
             sums = bank("ve", h, t)
@@ -333,7 +302,7 @@ def tile_list_dl_sigP_kernel(
             nc.vector.tensor_tensor(
                 out=y[h][:, t, c0 : c0 + width],
                 in0=ve[h, t][:, c0 : c0 + width],
-                in1=gate[h, t // 2][:, t % 2, c0 : c0 + width],
+                in1=gate[h][:, t, c0 : c0 + width],
                 op=MULT,
             )
 

@@ -58,9 +58,6 @@ def tile_list_dl_sigP_kernel(
         def tile(name, shape, dtype, tag=None):
             return sbuf.tile([P] + shape, dtype, name=name, tag=tag or name, align_bytes=MX_ALIGN)
 
-        offsets = sbuf.tile([P, J // LIST_ROWS], U16, name="offsets")
-        nc.sync.dma_start(offsets[:], offs)
-
         runs = J // P
         wgt_rows = tile("wgt_rows", [P], F32)
         nc.sync.dma_start(
@@ -117,6 +114,8 @@ def tile_list_dl_sigP_kernel(
             for u in range(2):
                 nc.sync.dma_start(out=st_sb[h, u][:], in_=st_rows[:, 2 * u : 2 * u + 2, h * HALF : (h + 1) * HALF])
 
+        offsets = sbuf.tile([P, J // LIST_ROWS], U16, name="offsets")
+        nc.sync.dma_start(offsets[:], offs)
         load_x(0, windows - 2)
         for a in range(PASSES):
             nc.sync.dma_start(out=wk_in[a][:], in_=wk_rows[a])
@@ -130,21 +129,22 @@ def tile_list_dl_sigP_kernel(
         turned = psum.tile([P, P], F32, name="turned", tag="bank0")
         nc.tensor.transpose(turned[:], wgt_rows[:], identity[:])
         by_head = turned[:, 0 : runs * HEADS].rearrange("p (g s) -> p s g", g=HEADS).unsqueeze(3)
-        half_runs = runs // 2
-        for h in range(2):
-            repeated = tile("repeated%d" % h, [half_runs, HEADS, LIST_ROWS], F32)
+        first_cuts = (0, QUARTER, HALF, J)
+        for n, (c0, c1) in enumerate(zip(first_cuts, first_cuts[1:])):
+            count = (c1 - c0) // P
+            repeated = tile("repeated%d" % n, [count, HEADS, LIST_ROWS], F32)
             nc.scalar.copy(
-                out=repeated[:],
-                in_=by_head[:, h * half_runs : (h + 1) * half_runs].to_broadcast([P, half_runs, HEADS, LIST_ROWS]),
+                out=repeated[:], in_=by_head[:, c0 // P : c1 // P].to_broadcast([P, count, HEADS, LIST_ROWS])
             )
-            back = psum.tile([P, half_runs, P], F32, name="back", tag="bank%d" % (1 + h))
-            for s in range(half_runs):
+            back = psum.tile([P, count, P], F32, name="back", tag="bank%d" % (1 + n))
+            for s in range(count):
                 nc.tensor.transpose(back[:, s, :], repeated[:, s].rearrange("p g r -> p (g r)"), identity[:])
-            nc.scalar.copy(out=wgt_sb[:, h * HALF : (h + 1) * HALF], in_=back[:].rearrange("p s c -> p (s c)"))
+            copy = nc.vector.tensor_copy if c1 <= HALF else nc.scalar.copy
+            copy(out=wgt_sb[:, c0:c1], in_=back[:].rearrange("p s c -> p (s c)"))
 
         def deal(copy, w_bf, columns, m0=0):
             copy(
-                out=w_bf[:].rearrange("p (t m i) -> p m i t", t=PACK, i=PACK)[:, m0 : m0 + columns.shape[2] // PACK],
+                out=w_bf.rearrange("p (t m i) -> p m i t", t=PACK, i=PACK)[:, m0 : m0 + columns.shape[2] // PACK],
                 in_=columns.rearrange("p i (m t) -> p m i t", t=PACK),
             )
 
@@ -206,8 +206,8 @@ def tile_list_dl_sigP_kernel(
         def bank(name, h, t):
             return psum.tile([P, HALF], F32, name=name, tag="bank%d" % (PACK * h + t))
 
-        for h in range(2):
-            pick(0, h * HALF, HALF)
+        for c0, c1 in zip(first_cuts, first_cuts[1:]):
+            pick(0, c0, c1 - c0)
         pick(1, 0, J)
         x_bf0 = tile("x_bf0", [PACK * J], BF16)
         for h in range(2):
@@ -223,20 +223,22 @@ def tile_list_dl_sigP_kernel(
         for h in range(2):
             x_mx[0, h] = (codes[:, h * HALF : (h + 1) * HALF].bitcast(FP8X4), scales[:, h * HALF : (h + 1) * HALF])
 
-        wk_bf = [tile("wk_bf%d" % a, [PACK * N], BF16) for a in range(PASSES)]
-        deal(nc.scalar.copy, wk_bf[0], wk_in[0][:])
-        x_bf[1, 0] = tile("x_bf10", [PACK * HALF], BF16, "wk_in0")[:]
+        wk0_bf = tile("wk0_bf", [PACK * N], BF16)
+        deal(nc.scalar.copy, wk0_bf[:], wk_in[0][:])
+        last_bf = tile("last_bf", [PACK * (N + HALF)], BF16, "wk_in0")
+        x_bf[1, 0] = last_bf[:, PACK * N :]
         round_pair(1, 0, 0)
-        deal(nc.scalar.copy, wk_bf[1], wk_in[1][:])
+        deal(nc.scalar.copy, last_bf[:, 0 : PACK * N], wk_in[1][:])
         pick(6, 0, HALF, last_pair[:, 0, :])
         pick(6, HALF, HALF)
-        wk_mx = [slices(*quantise("wk0", wk_bf[0][:], "x_in6"))]
+        wk_mx = [slices(*quantise("wk0", wk0_bf[:], "x_in6"))]
         for c0 in range(0, HALF, QUARTER):
             pick(7, c0, QUARTER, last_pair[:, 1, c0 : c0 + QUARTER])
             round_pair(1, 0, 1, c0, QUARTER, last_pair[:, :, c0 : c0 + QUARTER])
         pick(7, HALF, HALF)
-        wk_mx.append(slices(*quantise("wk1", wk_bf[1][:], "x_in7")))
-        quantise_x(1, 0)
+        codes, scales = quantise("last", last_bf[:])
+        wk_mx.append(slices(codes, scales))
+        x_mx[1, 0] = (codes[:, N:].bitcast(FP8X4), scales[:, N:])
         x_bf[1, 1] = tile("x_bf11", [PACK * HALF], BF16)[:]
         interleave(nc.scalar.copy, x_bf[1, 1], picked[1][:, :, HALF:J])
         v4_words = tile("v4_words", [PASSES, 2 * N], U8, "last_pair")
@@ -275,7 +277,7 @@ def tile_list_dl_sigP_kernel(
             logits(0, u)
         wd_mx = []
         for a in range(PASSES):
-            deal(nc.scalar.copy, wd_bf[a], wd_in[a][:])
+            deal(nc.scalar.copy, wd_bf[a][:], wd_in[a][:])
             if a == PASSES - 1:
                 logits(1, 0)
             wd_mx.append(slices(*quantise("wd%d" % a, wd_bf[a][:])))

@@ -192,13 +192,13 @@ def tile_list_dl_sigP_kernel(
             codes, scales = quantise("x%d%d" % (a, h), x_bf[a, h], tag)
             x_mx[a, h] = (codes[:].bitcast(FP8X4), scales)
 
-        def mx_pass(bank, w_slice, a, h, start, stop):
+        def mx_pass(out, w_slice, a, h, start, stop, places=slice(0, HALF)):
             nc.tensor.matmul_mx(
-                out=bank[:],
+                out=out,
                 lhsT=w_slice[0],
                 lhsT_scale=w_slice[1],
-                rhs=x_mx[a, h][0],
-                rhs_scale=x_mx[a, h][1],
+                rhs=x_mx[a, h][0][:, places],
+                rhs_scale=x_mx[a, h][1][:, places],
                 start=start,
                 stop=stop,
             )
@@ -259,7 +259,7 @@ def tile_list_dl_sigP_kernel(
         for h in range(2):
             for a in range(PASSES):
                 for t in range(PACK):
-                    mx_pass(ke[h, t], wk_mx[a][t], a, h, a == 0, a == PASSES - 1)
+                    mx_pass(ke[h, t][:], wk_mx[a][t], a, h, a == 0, a == PASSES - 1)
 
         gate = [tile("gate%d" % h, [PACK, HALF], F32, tag="wd_in%d" % (1 - h)) for h in range(2)]
 
@@ -286,30 +286,31 @@ def tile_list_dl_sigP_kernel(
             for u in range(2):
                 gates(h, u)
 
-        def value_passes(h, t):
-            sums = bank("ve", h, t)
+        def value_passes(out, h, t, places, late):
             terms = [(w[a][t], a) for w in (v4_mx, wd_mx) for a in range(PASSES)]
-            if (h, t // 2) == (1, 1):
+            if late:
                 terms = terms[::-1]
             for n, (w_slice, a) in enumerate(terms):
-                mx_pass(sums, w_slice, a, h, n == 0, n == len(terms) - 1)
-            return sums
+                mx_pass(out, w_slice, a, h, n == 0, n == len(terms) - 1, places)
+
+        parts = [(n // PACK, slice(n % PACK, n % PACK + 1), slice(0, HALF)) for n in range(2 * PACK - 2)]
+        parts += [(1, slice(2, PACK), slice(c0, c0 + QUARTER)) for c0 in range(0, HALF, QUARTER)]
+        ve = []
+        for n, (h, ts, places) in enumerate(parts):
+            sums = psum.tile([P, ts.stop - ts.start, places.stop - places.start], F32, name="ve", tag="bank%d" % n)
+            for t in range(ts.start, ts.stop):
+                value_passes(sums[:, t - ts.start, :], h, t, places, n >= 2 * PACK - 2)
+            ve.append(sums)
 
         y_codes = tile("y_codes", [J], U32)
         y_scales = tile("y_scales", [J], U8)
         words_out = out_1.rearrange("a p j i -> p (a j i)").bitcast(I32)
         y = [tile("y%d" % h, [PACK, HALF], F32, tag="x_in%d" % (1 + h)) for h in range(2)]
 
-        def result(h, t, c0, width):
-            nc.vector.tensor_tensor(
-                out=y[h][:, t, c0 : c0 + width],
-                in0=ve[h, t][:, c0 : c0 + width],
-                in1=gate[h][:, t, c0 : c0 + width],
-                op=MULT,
+        def store(h, ts, places):
+            nc.sync.dma_start(
+                out=out_rows[:, ts, h * HALF + places.start : h * HALF + places.stop], in_=y[h][:, ts, places]
             )
-
-        def store(h, part):
-            nc.sync.dma_start(out=out_rows[:, part, h * HALF : (h + 1) * HALF], in_=y[h][:, part, :])
 
         def rounded(name, h, c0, width, copies):
             share = width // len(copies)
@@ -320,26 +321,22 @@ def tile_list_dl_sigP_kernel(
                     y_bf[:, PACK * n * share : PACK * (n + 1) * share],
                     y[h][:, :, c0 + n * share : c0 + (n + 1) * share],
                 )
-            return y_bf
+            return y_bf, h * HALF + c0, width
 
         def planes(y_bf, c0, width):
             places = slice(c0, c0 + width)
             nc.vector.quantize_mx(out=y_codes[:, places].bitcast(FP8X4), scales=y_scales[:, places], in_=y_bf[:])
             nc.sync.dma_start(out=words_out[:, places], in_=y_codes[:, places].bitcast(I32))
 
-        ve = {(h, t): value_passes(h, t) for h in range(2) for t in range(PACK)}
-        for h in range(2):
-            for t in range(PACK):
-                width = QUARTER if (h, t) == (1, PACK - 1) else HALF
-                for c0 in range(0, HALF, width):
-                    result(h, t, c0, width)
-                if (h, t // 2) == (1, 1):
-                    store(h, slice(t, t + 1))
-                elif t % 2 == 1:
-                    store(h, slice(t - 1, t + 1))
-        pieces = [(rounded("y_bf0", 0, 0, HALF, [nc.scalar.copy, gpsimd_copy]), 0, HALF)]
-        for q, copy in enumerate((nc.scalar.copy, nc.vector.tensor_copy)):
-            pieces.append((rounded("y_bf%d" % (1 + q), 1, q * QUARTER, QUARTER, [copy]), HALF + q * QUARTER, QUARTER))
+        for sums, (h, ts, places) in zip(ve, parts):
+            nc.vector.tensor_tensor(out=y[h][:, ts, places], in0=sums[:], in1=gate[h][:, ts, places], op=MULT)
+            if ts.stop % 2 == 0:
+                store(h, slice(ts.stop - 2, ts.stop), places)
+        pieces = [
+            rounded("y_bf0", 0, 0, HALF, [nc.scalar.copy, gpsimd_copy]),
+            rounded("y_bf1", 1, 0, QUARTER, [nc.scalar.copy]),
+            rounded("y_bf2", 1, QUARTER, QUARTER, [nc.scalar.copy, nc.vector.tensor_copy]),
+        ]
         for piece in pieces:
             planes(*piece)
 

@@ -330,8 +330,7 @@ def tile_list_dl_sigP_kernel(
 
         for sums, (h, ts, places) in zip(ve, parts):
             nc.vector.tensor_tensor(out=y[h][:, ts, places], in0=sums[:], in1=gate[h][:, ts, places], op=MULT)
-            if ts.stop % 2 == 0:
-                store(h, slice(ts.stop - 2, ts.stop), places)
+            store(h, ts, places)
         pieces = [
             rounded("y_bf0", 0, 0, HALF, [nc.scalar.copy, gpsimd_copy]),
             rounded("y_bf1", 1, 0, QUARTER, [nc.scalar.copy]),

@@ -28,7 +28,7 @@ HEADS = P // LIST_ROWS
 LINE = 4
 HALF = J // 2
 QUARTER = J // 4
-MX_ALIGN = 64
+MX_ALIGN = 256
 
 
 def interleave(copy, out, rows):

from contextlib import ExitStack

import concourse.mybir as mybir
from concourse.masks import make_identity

K, N, T, J = 1024, 512, 2048, 1024
FLOPS = 3 * 2 * K * N * J

F32 = mybir.dt.float32
BF16 = mybir.dt.bfloat16
I32 = mybir.dt.int32
U32 = mybir.dt.uint32
U16 = mybir.dt.uint16
U8 = mybir.dt.uint8
FP8X4 = mybir.dt.float8_e4m3fn_x4
FP4X4 = mybir.dt.float4_e2m1fn_x4
MULT = mybir.AluOpType.mult
ADD = mybir.AluOpType.add
SIGMOID = mybir.ActivationFunctionType.Sigmoid

P = 128
PACK = 4
PASSES = K // (P * PACK)
QUADRANTS = 4
SCALE_ROWS = 4
LIST_ROWS = 16
HEADS = P // LIST_ROWS
LINE = 4
HALF = J // 2
QUARTER = J // 4
MX_ALIGN = 256


def interleave(copy, out, rows):
    copy(
        out=out.rearrange("p (b c i) -> p b i c", c=LINE, i=PACK),
        in_=rows.rearrange("p i (b c) -> p b i c", c=LINE),
    )


def scale_rows(quad):
    return slice(SCALE_ROWS * quad, SCALE_ROWS * (quad + 1))


def scale_partitions(quad):
    first = quad * (P // QUADRANTS)
    return slice(first, first + SCALE_ROWS)


def tile_list_dl_sigP_kernel(
    tc, xT, wgt, wk, wv4_words, wv4_scales, wvd, st, offs, out_0, out_1, out_2
):
    nc = tc.nc
    with ExitStack() as ctx:
        sbuf = ctx.enter_context(tc.tile_pool(name="sbuf", bufs=1))
        psum = ctx.enter_context(tc.psum_pool(name="psum", bufs=1))

        def tile(name, shape, dtype, tag=None):
            return sbuf.tile([P] + shape, dtype, name=name, tag=tag or name, align_bytes=MX_ALIGN)

        runs = J // P
        wgt_rows = tile("wgt_rows", [P], F32)
        nc.sync.dma_start(
            out=wgt_rows[0 : runs * HEADS, :],
            in_=wgt.rearrange("(g r) (s c) -> r g s c", r=LIST_ROWS, c=P)[0],
        )
        nc.vector.memset(wgt_rows[runs * HEADS : P, :], 0.0)
        identity = tile("identity", [P], F32)
        make_identity(nc, identity[:])

        v4_rows = tile("v4_rows", [PASSES, N], U8)
        v4_scales_in = tile("v4_scales_in", [PASSES, N], U8)
        v4_scales = tile("v4_scales", [PASSES, N], U8)
        nc.vector.memset(v4_scales_in[:].bitcast(I32), 0)
        for quad in range(QUADRANTS):
            queue = nc.sync if quad < QUADRANTS // 2 else nc.scalar
            queue.dma_start(
                out=v4_rows[scale_partitions(quad), :, :].bitcast(I32),
                in_=wv4_scales[:, scale_rows(quad), :].bitcast(I32).rearrange("a r w -> r a w"),
            )
            nc.vector.tensor_copy(
                out=v4_scales_in[scale_partitions(quad), :, :].bitcast(I32),
                in_=v4_rows[scale_partitions(quad), :, :].bitcast(I32),
            )
        nc.vector.tensor_copy(
            out=v4_scales[:].rearrange("p a (t m) -> p a t m", t=PACK),
            in_=v4_scales_in[:].rearrange("p a (m t) -> p a t m", t=PACK),
        )

        warm = tile("warm", [2], F32)
        nc.vector.memset(warm[:, 0:1], 0.0)
        nc.scalar.activation(out=warm[:, 1:2], in_=warm[:, 0:1], func=SIGMOID)

        windows = PASSES * PACK
        picked = [tile("picked%d" % a, [PACK, J], F32) for a in range(PASSES)]
        last_pair = tile("last_pair", [2, HALF], F32)
        wgt_sb = tile("wgt_sb", [J], F32)
        v4_words_in = tile("v4_words_in", [PASSES, 2 * N], U8)
        x_in = [tile("x_in%d" % r, [T], F32) for r in range(windows)]
        wk_in = [tile("wk_in%d" % a, [PACK, N], F32) for a in range(PASSES)]
        wd_in = [tile("wd_in%d" % a, [PACK, N], F32) for a in range(PASSES)]
        st_sb = {(h, u): tile("st_sb%d%d" % (h, u), [2, HALF], F32) for h in range(2) for u in range(2)}
        x_rows = xT.rearrange("(a p i) c -> a i p c", p=P, i=PACK)
        wk_rows = wk.rearrange("(a p i) n -> a p i n", p=P, i=PACK)
        wd_rows = wvd.rearrange("(a p i) n -> a p i n", p=P, i=PACK)
        st_rows = st.rearrange("(p t) j -> p t j", t=PACK)
        out_rows = out_0.rearrange("(p t) j -> p t j", t=PACK)

        def load_x(first, end):
            for r in range(first, end):
                nc.sync.dma_start(out=x_in[r][:], in_=x_rows[r // PACK, r % PACK])

        def load_st(h):
            for u in range(2):
                nc.sync.dma_start(out=st_sb[h, u][:], in_=st_rows[:, 2 * u : 2 * u + 2, h * HALF : (h + 1) * HALF])

        offsets = sbuf.tile([P, J // LIST_ROWS], U16, name="offsets")
        nc.sync.dma_start(offsets[:], offs)
        load_x(0, windows - 2)
        for a in range(PASSES):
            nc.sync.dma_start(out=wk_in[a][:], in_=wk_rows[a])
            load_x(windows - 2 + a, windows - 1 + a)
        nc.sync.dma_start(out=v4_words_in[:].bitcast(I32), in_=wv4_words.bitcast(I32).rearrange("a p w -> p a w"))
        load_st(0)
        nc.sync.dma_start(out=wd_in[0][:], in_=wd_rows[0])
        nc.sync.dma_start(out=wd_in[1][:], in_=wd_rows[1])
        load_st(1)

        turned = psum.tile([P, P], F32, name="turned", tag="bank0")
        nc.tensor.transpose(turned[:], wgt_rows[:], identity[:])
        by_head = turned[:, 0 : runs * HEADS].rearrange("p (g s) -> p s g", g=HEADS).unsqueeze(3)
        first_cuts = (0, QUARTER, HALF, J)
        for n, (c0, c1) in enumerate(zip(first_cuts, first_cuts[1:])):
            count = (c1 - c0) // P
            repeated = tile("repeated%d" % n, [count, HEADS, LIST_ROWS], F32)
            nc.scalar.copy(
                out=repeated[:], in_=by_head[:, c0 // P : c1 // P].to_broadcast([P, count, HEADS, LIST_ROWS])
            )
            back = psum.tile([P, count, P], F32, name="back", tag="bank%d" % (1 + n))
            for s in range(count):
                nc.tensor.transpose(back[:, s, :], repeated[:, s].rearrange("p g r -> p (g r)"), identity[:])
            copy = nc.vector.tensor_copy if c1 <= HALF else nc.scalar.copy
            copy(out=wgt_sb[:, c0:c1], in_=back[:].rearrange("p s c -> p (s c)"))

        def deal(copy, w_bf, columns, m0=0):
            copy(
                out=w_bf.rearrange("p (t m i) -> p m i t", t=PACK, i=PACK)[:, m0 : m0 + columns.shape[2] // PACK],
                in_=columns.rearrange("p i (m t) -> p m i t", t=PACK),
            )

        def quantise(name, values, tag=None):
            width = values.shape[1] // PACK
            codes = tile(name + "_codes", [width], U32, tag)
            scales = tile(name + "_scales", [width], U8)[:]
            nc.vector.quantize_mx(out=codes[:].bitcast(FP8X4), scales=scales, in_=values)
            return codes, scales

        def slices(codes, scales):
            return [(codes[:, P * t : P * (t + 1)].bitcast(FP8X4), scales[:, P * t : P * (t + 1)]) for t in range(PACK)]


        def pick(r, c0, width, out=None):
            nc.vector.tensor_tensor(
                out=picked[r // PACK][:, r % PACK, c0 : c0 + width] if out is None else out,
                in0=x_in[r][:].indirect(offsets[:, c0 // LIST_ROWS : (c0 + width) // LIST_ROWS]),
                in1=wgt_sb[:, c0 : c0 + width],
                op=MULT,
            )

        def gpsimd_copy(out, in_):
            nc.gpsimd.tensor_scalar(
                out=out.rearrange("p b i c -> p b c i"),
                in0=in_.rearrange("p b i c -> p b c i"),
                scalar1=1.0,
                scalar2=-0.0,
                op0=MULT,
                op1=ADD,
            )

        x_bf = {}
        x_mx = {}

        def round_pair(a, h, u, c0=0, width=HALF, pair=None):
            if pair is None:
                pair = picked[a][:, 2 * u : 2 * u + 2, h * HALF + c0 : h * HALF + c0 + width]
            nc.scalar.copy(
                out=x_bf[a, h].rearrange("p (c i) -> p c i", i=PACK)[:, c0 : c0 + width, 2 * u : 2 * u + 2],
                in_=pair.rearrange("p i c -> p c i"),
            )

        def quantise_x(a, h, tag=None):
            codes, scales = quantise("x%d%d" % (a, h), x_bf[a, h], tag)
            x_mx[a, h] = (codes[:].bitcast(FP8X4), scales)

        def mx_pass(out, w_slice, a, h, start, stop, places=slice(0, HALF)):
            nc.tensor.matmul_mx(
                out=out,
                lhsT=w_slice[0],
                lhsT_scale=w_slice[1],
                rhs=x_mx[a, h][0][:, places],
                rhs_scale=x_mx[a, h][1][:, places],
                start=start,
                stop=stop,
            )

        def bank(name, h, t):
            return psum.tile([P, HALF], F32, name=name, tag="bank%d" % (PACK * h + t))

        for c0, c1 in zip(first_cuts, first_cuts[1:]):
            pick(0, c0, c1 - c0)
        pick(1, 0, J)
        x_bf0 = tile("x_bf0", [PACK * J], BF16)
        for h in range(2):
            x_bf[0, h] = x_bf0[:, h * PACK * HALF : (h + 1) * PACK * HALF]
            round_pair(0, h, 0)
        pick(2, 0, J)
        pick(3, 0, J)
        for h in range(2):
            round_pair(0, h, 1)
        pick(4, 0, J)
        pick(5, 0, J)
        codes, scales = quantise("x0", x_bf0[:], "x_in5")
        for h in range(2):
            x_mx[0, h] = (codes[:, h * HALF : (h + 1) * HALF].bitcast(FP8X4), scales[:, h * HALF : (h + 1) * HALF])

        wk0_bf = tile("wk0_bf", [PACK * N], BF16)
        deal(nc.scalar.copy, wk0_bf[:], wk_in[0][:])
        last_bf = tile("last_bf", [PACK * (N + HALF)], BF16, "wk_in0")
        x_bf[1, 0] = last_bf[:, PACK * N :]
        round_pair(1, 0, 0)
        deal(nc.scalar.copy, last_bf[:, 0 : PACK * N], wk_in[1][:])
        pick(6, 0, HALF, last_pair[:, 0, :])
        pick(6, HALF, HALF)
        wk_mx = [slices(*quantise("wk0", wk0_bf[:], "x_in6"))]
        for c0 in range(0, HALF, QUARTER):
            pick(7, c0, QUARTER, last_pair[:, 1, c0 : c0 + QUARTER])
            round_pair(1, 0, 1, c0, QUARTER, last_pair[:, :, c0 : c0 + QUARTER])
        pick(7, HALF, HALF)
        codes, scales = quantise("last", last_bf[:])
        wk_mx.append(slices(codes, scales))
        x_mx[1, 0] = (codes[:, N:].bitcast(FP8X4), scales[:, N:])
        x_bf[1, 1] = tile("x_bf11", [PACK * HALF], BF16)[:]
        interleave(nc.scalar.copy, x_bf[1, 1], picked[1][:, :, HALF:J])
        v4_words = tile("v4_words", [PASSES, 2 * N], U8, "last_pair")
        nc.vector.tensor_copy(
            out=v4_words[:].bitcast(U16).rearrange("p a (t m) -> p a t m", t=PACK),
            in_=v4_words_in[:].bitcast(U16).rearrange("p a (m t) -> p a t m", t=PACK),
        )
        v4_mx = [
            [
                (v4_words[:, a, 2 * P * t : 2 * P * (t + 1)].bitcast(FP4X4), v4_scales[:, a, P * t : P * (t + 1)])
                for t in range(PACK)
            ]
            for a in range(PASSES)
        ]
        quantise_x(1, 1)

        ke = {(h, t): bank("ke", h, t) for h in range(2) for t in range(PACK)}
        for h in range(2):
            for a in range(PASSES):
                for t in range(PACK):
                    mx_pass(ke[h, t][:], wk_mx[a][t], a, h, a == 0, a == PASSES - 1)

        gate = [tile("gate%d" % h, [PACK, HALF], F32, tag="wd_in%d" % (1 - h)) for h in range(2)]

        def logits(h, u):
            for v in range(2):
                nc.vector.tensor_tensor(
                    out=st_sb[h, u][:, v, :], in0=ke[h, 2 * u + v][:], in1=st_sb[h, u][:, v, :], op=MULT
                )

        def gates(h, u):
            nc.scalar.activation(out=gate[h][:, 2 * u : 2 * u + 2, :], in_=st_sb[h, u][:], func=SIGMOID)

        wd_bf = [tile("wd_bf%d" % a, [PACK * N], BF16) for a in range(PASSES)]
        for u in range(2):
            logits(0, u)
        wd_mx = []
        for a in range(PASSES):
            deal(nc.scalar.copy, wd_bf[a][:], wd_in[a][:])
            if a == PASSES - 1:
                logits(1, 0)
            wd_mx.append(slices(*quantise("wd%d" % a, wd_bf[a][:])))
        logits(1, 1)
        for h in range(2):
            for u in range(2):
                gates(h, u)

        def value_passes(out, h, t, places, late):
            terms = [(w[a][t], a) for w in (v4_mx, wd_mx) for a in range(PASSES)]
            if late:
                terms = terms[::-1]
            for n, (w_slice, a) in enumerate(terms):
                mx_pass(out, w_slice, a, h, n == 0, n == len(terms) - 1, places)

        parts = [(n // PACK, slice(n % PACK, n % PACK + 1), slice(0, HALF)) for n in range(2 * PACK - 2)]
        parts += [(1, slice(2, PACK), slice(c0, c0 + QUARTER)) for c0 in range(0, HALF, QUARTER)]
        ve = []
        for n, (h, ts, places) in enumerate(parts):
            sums = psum.tile([P, ts.stop - ts.start, places.stop - places.start], F32, name="ve", tag="bank%d" % n)
            for t in range(ts.start, ts.stop):
                value_passes(sums[:, t - ts.start, :], h, t, places, n >= 2 * PACK - 2)
            ve.append(sums)

        y_codes = tile("y_codes", [J], U32)
        y_scales = tile("y_scales", [J], U8)
        words_out = out_1.rearrange("a p j i -> p (a j i)").bitcast(I32)
        y = [tile("y%d" % h, [PACK, HALF], F32, tag="x_in%d" % (1 + h)) for h in range(2)]

        def store(h, ts, places):
            nc.sync.dma_start(
                out=out_rows[:, ts, h * HALF + places.start : h * HALF + places.stop], in_=y[h][:, ts, places]
            )

        def rounded(name, h, c0, width, copies):
            share = width // len(copies)
            y_bf = tile(name, [PACK * width], BF16)
            for n, copy in enumerate(copies):
                interleave(
                    copy,
                    y_bf[:, PACK * n * share : PACK * (n + 1) * share],
                    y[h][:, :, c0 + n * share : c0 + (n + 1) * share],
                )
            return y_bf, h * HALF + c0, width

        def planes(y_bf, c0, width):
            places = slice(c0, c0 + width)
            nc.vector.quantize_mx(out=y_codes[:, places].bitcast(FP8X4), scales=y_scales[:, places], in_=y_bf[:])
            nc.sync.dma_start(out=words_out[:, places], in_=y_codes[:, places].bitcast(I32))

        for sums, (h, ts, places) in zip(ve, parts):
            nc.vector.tensor_tensor(out=y[h][:, ts, places], in0=sums[:], in1=gate[h][:, ts, places], op=MULT)
            store(h, ts, places)
        pieces = [
            rounded("y_bf0", 0, 0, HALF, [nc.scalar.copy, gpsimd_copy]),
            rounded("y_bf1", 1, 0, QUARTER, [nc.scalar.copy]),
            rounded("y_bf2", 1, QUARTER, QUARTER, [nc.scalar.copy, nc.vector.tensor_copy]),
        ]
        for piece in pieces:
            planes(*piece)

        for quad in range(QUADRANTS):
            queue = nc.sync if quad % 2 == 0 else nc.scalar
            queue.dma_start(
                out=out_2[0, scale_rows(quad), :].bitcast(I32),
                in_=y_scales[scale_partitions(quad), :].bitcast(I32),
            )
